import numpy as np, ml_dtypes
CORES = [36,164,52,180,100,228,116,244]
N = 8
import mx_ref
BF = ml_dtypes.bfloat16
def pick(q, e):
    c = np.concatenate([q[0].reshape(128, -1, 4), np.zeros((128, 1, 4), np.uint8)], axis=1); s = np.concatenate([q[1], np.ones((16, 1), np.uint8)], axis=1)
    return (np.ascontiguousarray(c[:, e].reshape(128, -1)), np.ascontiguousarray(s[:, e]))
def join(*qs):
    return (np.concatenate([q[0] for q in qs], axis=1), np.concatenate([q[1] for q in qs], axis=1))
def put(q, e, v):
    c, s = q[0].reshape(128, -1, 4).copy(), q[1].copy(); c[:, e] = v[0].reshape(128, -1, 4); s[:, e] = v[1]
    return (c.reshape(128, -1), s)
def pk(c, s):
    return (np.ascontiguousarray(c), mx_ref.live(s))
def emit(q):
    return q[0], q[1]
def packed(v, rng):
    q = [mx_ref.quantize(np.ascontiguousarray(v[r])) for r in range(N)]
    return np.stack([a for a, b in q]), np.stack([mx_ref.plane(b, rng) for a, b in q])
def values_of_codes():
    e, c = np.zeros((128, 128, 4), np.float32), np.zeros((128, 2, 4), np.uint8)
    e[np.arange(128), np.arange(128), 0] = 1
    c[:127, :, 0] = np.arange(256).reshape(2, 128).T[:127]
    return mx_ref.matmul(mx_ref.quantize(e.reshape(128, 512).astype(BF)), (c.reshape(128, 8), np.full((16, 2), 127, np.uint8))).T.reshape(-1).astype(np.float64)
CODE_VALUE, SCALE_VALUE = values_of_codes(), 2.0 ** (np.arange(256) - 127.0)
def decode(q):
    return (CODE_VALUE[q[0]].reshape(16, 8, -1, 4) * SCALE_VALUE[q[1]][:, None, :, None] + 0.0).reshape(128, -1).astype(np.float32)
def f(rng, *shape):
    return mx_ref.flush((rng.standard_normal(shape, dtype=np.float32) * np.exp2(rng.integers(-2, 3, shape[:-1] + (1,)))).astype(BF))
def wide(rng, *shape, cols=0):
    v = rng.standard_normal(shape, dtype=np.float32) * np.exp2(rng.integers(-12, 13, shape)).astype(np.float32)
    if cols: v *= np.repeat(np.exp2(rng.integers(-cols, cols + 1, shape[:-2] + (1, shape[-1] // 4))) * (rng.random(shape[:-2] + (1, shape[-1] // 4)) > 0.0625), 4, axis=-1).astype(np.float32)
    return mx_ref.flush(v.astype(BF))
C, L, R = 320, 40, 3
def match(p):
    s = np.array(p.reshape(8, 16, C)[:, :8].transpose(2, 0, 1) + np.float32(0.0), order="C")
    j = np.arange(C)
    g = np.zeros((8, C), np.int64)
    for k in range(8):
        e = np.argmax(s.reshape(C, 64), axis=1)
        g[e % 8, j] = e // 8
        s[j, e // 8] = -np.inf
        s[j, :, e % 8] = -np.inf
    return g
def order(p, g):
    m = p[16 * g + np.arange(8)[:, None], np.arange(C)]
    return np.argsort(-(m + np.float32(0.0)), axis=1, kind="stable")
def sung(t, g, o):
    b = t.reshape(8, 16, C, 4)[np.take_along_axis(g, o, axis=1), :, o]
    return np.ascontiguousarray(b.transpose(0, 2, 1, 3)).reshape(128, -1)
def numbers_of(rng):
    return {"x": np.array(f(rng, N, 128, 4 * C)), "u": np.array(f(rng, N, 128, 512)), "v": np.array(f(rng, N, 128, 512))}
def weights(rng, w):
    c, p = packed(w, rng)
    return {"wc": c, "ws": p}
def still(rng):
    return weights(rng, np.zeros((N, 128, 2048), BF))
def setup_inputs(rng):
    return {**numbers_of(rng), **weights(rng, f(rng, N, 128, 2048))}
def setup_inputs_ties(rng):
    d = numbers_of(rng)
    e = rng.permutation(N)
    x = d["x"].reshape(N, 8, 16, C, 4)
    u = d["u"].reshape(N, 8, 16, 128, 4)
    for r in range(N):
        k = np.zeros(C, int) if r == e[2] else rng.permutation(C) % 3
        a = x[r][:, :8, :3].copy()
        a[:, :, 2] = 0
        x[r][:, :8] = a[:, :, k]
        i = np.ones((8, 16), int)
        i[np.arange(8), rng.permutation(8)] = 0
        if r == e[0]: i[:] = 0
        a = u[r][:, :8, :2].copy()
        u[r][:, :8] = a[:, :, i.reshape(-1)]
    x[e[1]] = 0
    u[:, :, 8:] = 0
    w = np.array(f(rng, N, 128, 2048)).reshape(N, 8, 16, 4, 8, 16, 4)
    w[:, :, 8:, :, :, :8] = 0
    return {"x": x.reshape(N, 128, 4 * C), "u": u.reshape(N, 128, 512), "v": d["v"], **weights(rng, w.reshape(N, 128, 2048))}
def setup_inputs_near(rng):
    d = numbers_of(rng)
    turned = np.argsort(rng.random((N, 8)), axis=1) + 8 * rng.integers(0, 32, (N, 8))
    s = (np.arange(C) // 2) ^ turned[:, :, None]
    a = np.stack([rng.permutation([1.0, 1.0, 1.0, -1.0, -1.0, -1.0, 0.0, 0.0]) for r in range(N)])
    x = (rng.integers(4, 8, (N, 8, 16, C, 4)) * rng.choice([-1.0, 1.0], (N, 8, 16, C, 4))).astype(np.float32)
    x[:, :, :8] *= np.float32(2.0 ** -9)
    x[:, :, 8:] *= np.float32(2.0 ** -27)
    x[:, :, 0] = 0
    x[:, :, 0, :, 0] = a[:, :, None] * 2.0 ** -7
    b = ((s[..., None] >> np.arange(8)) & 1) * np.exp2(np.arange(8) - 30.0)
    x[:, :, 8] = b[..., :4]
    x[:, :, 9] = b[..., 4:]
    c = 4 + np.repeat(rng.integers(0, 2, (N, 8, C // 2, 4)), 2, axis=2) + (np.arange(C) % 2)[:, None]
    x[:, :, 11] = (a == 0)[:, :, None, None] * c * 2.0 ** -32
    for r in range(N):
        x[r, rng.permutation(8)[:4], 0, int(rng.integers(C)), 0] = np.array([1.0, 1.0, -1.0, -1.0]) * 2.0 ** 30
    u = d["u"].reshape(N, 128, 128, 4)
    k = np.where(rng.permutation(N) < N // 2, 2.0 ** -30, 1.0).astype(np.float32).astype(BF)
    for g in range(8):
        for h in range(8):
            u[:, :, 16 * g + h] = 0
            u[:, 16 * g, 16 * g + h, 0] = k
            u[:, 16 * g + 8:16 * g + 10, 16 * g + h] = k[:, None, None]
            u[:, 16 * g + 8 + h // 4, 16 * g + h, h % 4] = 0
            u[:, 16 * g + 11, 16 * g + h, h % 4] = k
    return {"x": x.reshape(N, 128, 4 * C).astype(BF), "u": u.reshape(N, 128, 512), "v": d["v"], **still(rng)}
def setup_inputs_huge(rng):
    d = numbers_of(rng)
    o = rng.permutation(N) % 4
    c, a = np.ones((N, C)), np.ones((N, 128))
    for r in range(N):
        if o[r] == 0: a[r] = -1
        if o[r] == 2: c[r] = rng.permutation(C) % 2 * 2.0 - 1.0
        if o[r] == 3: a[r] = rng.permutation(128) % 2 * 2.0 - 1.0
    x = 2.0 ** 30 * (0.6 + 0.4 * rng.random((N, 128, C, 4))) * c[:, None, :, None]
    u = 2.0 ** 30 * (1 - 0.25 * rng.random((N, 128, 128, 4))) * a[:, None, :, None]
    return {"x": x.astype(np.float32).reshape(N, 128, 4 * C).astype(BF), "u": u.astype(np.float32).reshape(N, 128, 512).astype(BF), "v": d["v"], **still(rng)}
def setup_inputs_spread(rng):
    d = setup_inputs(rng)
    d["x"] = wide(rng, N, 128, 4 * C, cols=6)
    return d
def check_inputs(d):
    b = []
    for k in ("x", "u", "v"):
        a = np.abs(d[k].astype(np.float32))
        if not (np.isfinite(a).all() and ((a == 0) | (a >= 2.0 ** -30) & (a <= 2.0 ** 30)).all()): b.append("a value of " + k)
    if np.isin(d["wc"], (127, 255)).any(): b.append("a code of wc")
    none, low, high = [int(mx_ref.quantize(np.full((128, 16), k, np.float32).astype(BF))[1].max()) for k in (0.0, 2.0 ** -30, 2.0 ** 30)]
    s = np.stack([mx_ref.live(p) for p in d["ws"]])
    if not ((s == none) | (s >= low) & (s <= high)).all(): b.append("a scale of ws")
    return b
def reference(x, u, v, wc, ws):
    qu = [mx_ref.quantize(u[r]) for r in range(N)]
    lay = [pk(wc[r], ws[r]) for r in range(N)]
    now = [mx_ref.quantize(x[r]) for r in range(N)]
    for t in range(R):
        g, o, sent = [], [], []
        for r in range(N):
            p = mx_ref.matmul(qu[r], now[r])
            g.append(match(p))
            o.append(order(p, g[r]))
            sent.append(mx_ref.quantize(sung(decode(now[r]).astype(BF), g[r], o[r])))
        for r in range(N):
            m = join(*[pick(sent[s], np.arange(L * r, L * r + L)) for s in range(N)])
            z = np.stack([np.maximum(mx_ref.matmul(pick(lay[r], np.arange(128 * b, 128 * b + 128)), m), np.float32(0.0)) * np.float32(0.03125) for b in range(4)], axis=2)
            now[r] = mx_ref.quantize((decode(m) + z.reshape(128, -1)).astype(BF))
    y, ol = np.zeros((N, 128, C), np.float32), np.zeros((N, 8, 2 * C), np.float32)
    oc, osc = np.zeros((N, 128, 4 * C), np.uint8), np.zeros((N, 16, C), np.uint8)
    for r in range(N):
        y[r] = mx_ref.matmul(mx_ref.quantize(v[r]), now[r])
        ol[r] = np.concatenate([o[r], g[r]], axis=1)
        oc[r], osc[r] = emit(now[r])
    return {"y": y, "ol": ol, "oc": oc, "osc": osc}

@@ -1,0 +1,365 @@
+from concourse.bass import DstId, RemoteDMATransfer
+from concourse.mybir import dt, AluOpType, ActivationFunctionType
+
+C, L, ROUNDS, N = 320, 40, 3, 8
+NA = 8
+NV = 20 - NA
+ALIVE, DEAD, LOWEST = 2.0 ** 90, 2.0 ** 80, -(2.0 ** 95)
+_B = {
+    "bfloat16": dict(x0=4 * C, ut=512, vt=512, xs=4 * C, ones=512, et=4096, dp=4 * C, wd=32 * C, bt=4 * C, htab=64, gtab=64,
+                     tri=C, lt=192, fl=768, cap=384, eq=C, cor=C, fv=NV * C, so=NV * 160, sn=NA * C),
+    "float32": dict(rr=4 * C, neg=64, keep=192, pf=16, jcol=4, o1i=20, utab=20, o2f=20, o3f=2, base=20, pm=384, ee=24, ng=24,
+                    sa=192, sb=192, sk=192, gk=192, ss=256, sg=192, ta=64, zs=256, zv=128, zb=C, row=C, lb=C, zc=C, val=C,
+                    cb=20, a1=NA, a2=NA, a3=NA, rk=20, wo=352, tt=2 * C, t1=336, t3=336, oo=336, g1=C, g3=C, yo=C),
+    "int32": dict(pi=8, t2=336, g2=C),
+    "uint16": dict(off1=20, off2=20, off3=2, offr=20, offb=32),
+    "float8_e4m3fn_x4": dict(qu=128, qv=128, qw=512, qt=C, qe=1024, qb0=C, qb1=C, qb2=C, qm0=C, qm1=C, qm2=C),
+    "uint8": dict(su=128, sv=128, sw=512, st=C, se=1024, sq0=C, sq1=C, sq2=C, sm0=C, sm1=C, sm2=C),
+}
+SCRATCH = {k: ("sbuf", [128, n], d) for d, bufs in _B.items() for k, n in bufs.items()}
+SCRATCH["ps"] = ("psum", [128, 4096], "float32")
+SEMAPHORES = (["cv", "ca", "cp", "cg", "lx", "lu1", "lu2", "lw", "lv", "ol1", "ol2", "oy", "oq"]
+              + ["%s%d" % (a, t) for a in ("rep", "own", "snd", "arr") for t in range(ROUNDS)])
+
+A = AluOpType
+F = ActivationFunctionType
+HOP_SAME, HOP_CROSS = 70, 110
+STAGGER = 400
+CH = (0, 128, 192)
+
+
+def rank_program(g, core, T, topo):
+    rank = T.rank_of(core)
+    if rank is None:
+        return
+    V, S, P, Y = g.vector, g.scalar, g.tensor, g.sync
+    queue = {"v": V, "a": S, "p": P, "g": g, "y": Y}
+    ops, writer, readers, early, mms = [], {}, {}, [0], []
+
+    def op(eng, cost, fn, r=(), w=(), sem=None, inc=0, lat=0, after=(), soft=()):
+        deps = set(after) | {writer[k] for k in list(r) + list(w) if k in writer}
+        for k in w:
+            deps.update(readers.get(k, ()))
+        i = len(ops)
+        for k in r:
+            readers.setdefault(k, []).append(i)
+        for k in w:
+            writer[k] = i
+            readers[k] = []
+        ops.append({"eng": eng, "cost": cost, "fn": fn, "deps": deps, "sem": sem, "inc": inc,
+                    "early": early[0], "soft": set(soft), "lat": lat})
+        return i
+
+    def v(n, fn, r, w):
+        return op("v", max(64, n) + 8, fn, r, w)
+
+    def a(n, fn, r, w):
+        return op("a", max(78, n) + 8, fn, r, w)
+
+    def dma(eng, sem, pairs, r, w, lat):
+        def fn():
+            for o, i in pairs:
+                queue[eng].dma_start(o, i).then_inc(T.sem[sem], 16)
+        return op(eng, 100 * len(pairs), fn, r, w, sem=sem, inc=16 * len(pairs), lat=lat)
+
+    def mm(n, lq, ls, rq, rs, r):
+        bank = len(mms) % 8
+        out = T.ps[:, 512 * bank:512 * bank + n]
+        mms.append(op("p", 1.3 * n + 60, lambda: P.matmul_mx(out, lq, ls, rq, rs, True, True), r, ["b%d" % bank], soft=mms[-1:]))
+        return out, "b%d" % bank, 512 * bank
+
+    def quant(q, s, src, n, r, w):
+        op("v", 20 + 1.1 * n, lambda: V.quantize_mx(q, s, src), r, w)
+
+    def ts(out, in0, s1, s2, *o):
+        return lambda: V.tensor_scalar(out, in0, s1, s2, *o)
+
+    def tt(out, i0, i1, o):
+        return lambda: V.tensor_tensor(out, i0, i1, o)
+
+    def cp(out, in_):
+        return lambda: V.tensor_copy(out, in_)
+
+    def act(out, in_, func=F.Copy, **kw):
+        return lambda: S.activation(out, in_, func, **kw)
+
+    def scan(out, d0, d1, init, o0, o1):
+        return lambda: V.tensor_tensor_scan(out, d0, d1, init, o0, o1)
+
+    def tr(out, in_):
+        return lambda: V.transpose(out, in_)
+
+    def fill(out, x):
+        return lambda: V.memset(out, x)
+
+    def iota(out, pat, base, cm, n, w, **kw):
+        op("g", 160 + 2 * n, lambda: g.iota(out, pat, base, cm, **kw), [], w)
+
+    def fiota(out, pat, base, cm, n, w):
+        iota(out, pat, base, cm, n, w, allow_small_or_imprecise_dtypes=True)
+
+    def u8(view):
+        return view.bitcast(dt.uint8)
+
+    def blk(buf, k, n):
+        return buf[:, n * k:n * k + n]
+
+    dma("y", "lx", [(T.x0[:], T.x[:])], [], ["x0"], 3200)
+    uc = [(blk(T.ut, k, 32), T.u[:, 64 * k:64 * k + 32]) for k in range(8)]
+    dma("a", "lu1", uc[:5], [], ["ut1"], 2600)
+    dma("y", "lu2", uc[5:] + [(T.ut[:, 256:512], T.u[:, 0:256])], [], ["ut2"], 2600)
+    dma("y", "lw", [(u8(T.qw[:]), T.wc[:]), (T.sw[:], T.ws[:])], [], ["w"], 3000)
+    dma("y", "lv", [(T.vt[:], T.v[:])], [], ["vt"], 2600)
+    quant(T.qt[:], T.st[:], T.x0[:], C, ["x0"], ["t"])
+    quant(T.qu[:], T.su[:], T.ut[:], 128, ["ut1", "ut2"], ["u"])
+    quant(T.qv[:], T.sv[:], T.vt[:], 128, ["vt"], ["v"])
+
+    fiota(T.htab[:], [[0, 8], [1, 8]], 0, 0, 64, ["htab"])
+    fiota(T.gtab[:], [[-8, 8], [0, 8]], 0, 0, 64, ["gtab"])
+    v(64, fill(T.neg[:], LOWEST), [], ["neg"])
+    v(256, fill(T.ones[:], 1.0), [], ["ones"])
+    for e in range(8):
+        pat = [[4, 16], [64, 8], [1, 4]] if e < 4 else [[1, 512]]
+        op("g", 1224, (lambda e=e, pat=pat: g.affine_select(blk(T.et, e, 512), T.ones[:], pat, A.is_equal, 0.0, -(e % 4), -4)),
+           ["ones"], ["et%d" % e])
+        quant(blk(T.qe, e, 128), blk(T.se, e, 128), blk(T.et, e, 512), 128, ["et%d" % e], ["e%d" % e])
+    fiota(T.keep[:], [[0, 24], [1, 8]], 0, 0, 192, ["keep"])
+    v(192, ts(T.keep[:], T.keep[:], 0.0, None, A.is_gt), ["keep"], ["keep"])
+    iota(T.pi[:, 0:1], [[0, 1]], 0, 1, 1, ["pi0"])
+    v(1, ts(T.pi[:, 1:2], T.pi[:, 0:1], 1, None, A.bitwise_and), ["pi0"], ["pi1"])
+    v(1, ts(T.pi[:, 2:3], T.pi[:, 0:1], 15, None, A.bitwise_and), ["pi0"], ["pi2"])
+    v(1, ts(T.pi[:, 3:4], T.pi[:, 0:1], 4, 1, A.logical_shift_right, A.bitwise_and), ["pi0"], ["pi3"])
+    v(4, cp(T.pf[:, 0:4], T.pi[:, 0:4]), ["pi0", "pi1", "pi2", "pi3"], ["pf"])
+    pu, pl, ph = T.pf[:, 1:2], T.pf[:, 2:3], T.pf[:, 3:4]
+    v(1, ts(T.pf[:, 4:5], ph, -256.0, 127.0, A.mult, A.add), ["pf"], ["pf4"])
+    v(1, ts(T.pf[:, 5:6], ph, 129.0, None, A.mult), ["pf"], ["pf5"])
+    v(1, ts(T.pf[:, 6:7], ph, 16.0, None, A.mult), ["pf"], ["pf6"])
+    v(1, ts(T.pf[:, 7:8], pl, ph, 16.0, A.add, A.mult), ["pf"], ["pf7"])
+    v(1, ts(T.o3f[:, 0:1], pu, 304.0, T.pf[:, 7:8], A.mult, A.add), ["pf", "pf7"], ["o3a"])
+    v(1, ts(T.o3f[:, 1:2], T.o3f[:, 0:1], 256.0, 639.0, A.add, A.min), ["o3a"], ["o3b"])
+    v(2, cp(T.off3[:], T.o3f[:]), ["o3a", "o3b"], ["off3"])
+    fiota(T.jcol[:, 0:2], [[128, 2]], 0, 1, 2, ["j0"])
+    fiota(T.jcol[:, 2:3], [[0, 1]], CH[2], 1, 1, ["j1"])
+    o1 = []
+    for q in range(4):
+        q1, q0 = q >> 1, q & 1
+        s1, s0 = 32 - 64 * q1, 64 - 128 * q0
+        for c in range(3):
+            o1.append("o1_%d_%d" % (q, c))
+            if c < 2:
+                fiota(T.o1i[32 * q:32 * q + 32, 8 * c:8 * c + 8], [[s1, 2], [s0, 2], [1, 2]],
+                      32 * q1 + 64 * q0 + 8 * c + 2 * q, 0, 8, o1[-1:])
+            else:
+                fiota(T.o1i[32 * q:32 * q + 32, 16:20], [[s0, 2], [1, 2]], 32 * (1 - q1) + 64 * q0 + 16 + 2 * q, 0, 4, o1[-1:])
+    v(20, cp(T.off1[:], T.o1i[:]), o1, ["off1"])
+    fiota(T.utab[:], [[0, 10], [1, 2]], 0, 0, 20, ["utab"])
+    v(20, ts(T.utab[:], T.utab[:], T.pf[:, 4:5], T.pf[:, 5:6], A.mult, A.add), ["utab", "pf4", "pf5"], ["utab"])
+    v(40, tt(T.o2f[:], T.utab[:], T.o1i[:], A.add), o1 + ["utab"], ["o2f"])
+    v(20, cp(T.off2[:], T.o2f[:]), ["o2f"], ["off2"])
+    fiota(T.base[:, 0:NA], [[16, NA]], 15, 0, NA, ["base0"])
+    fiota(T.base[:, NA:20], [[0, NV]], 159, 0, NV, ["base1"])
+    v(20, ts(T.base[:], T.base[:], T.pf[:, 6:7], None, A.add), ["base0", "base1", "pf6"], ["base0", "base1"])
+    fiota(T.tri[:], [[0, 20], [1, 16]], 0, 0, C, ["tri"])
+    v(160, ts(T.tri[:], T.tri[:], pl, None, A.is_gt), ["tri", "pf"], ["tri"])
+    v(64, fill(T.ss[:, 192:256], 0.0), [], ["sspad"])
+    v(32, fill(T.zv[:, 24:32], 0.0), [], ["zvpad"])
+    v(352, fill(T.wo[:], 0.0), [], ["wo"])
+
+    def spread(eng, buf, c0, name, src, rs):
+        put, mk = (v, cp) if eng == "v" else (a, act)
+        for lo in (0, 64):
+            put(32, mk(buf[64 - lo:128 - lo, c0 + 32:c0 + 64], src(lo, lo + 64)), rs, ["%s_2_%d" % (name, 64 - lo)])
+        for q in range(4):
+            lo, hi = 32 * q, 32 * (q ^ 1)
+            put(64, mk(buf[hi:hi + 32, c0 + 64:c0 + 128], buf[lo:lo + 32, c0:c0 + 64]),
+                [name + "_0", "%s_2_%d" % (name, 64 * (q >> 1))], ["%s_1_%d" % (name, q ^ 1)])
+        return [name + "_0", name + "_2_0", name + "_2_64"] + ["%s_1_%d" % (name, q) for q in range(4)]
+
+    for t in range(ROUNDS):
+        lik = [mm(128, T.qt[:, lo:lo + 128], T.st[:, lo:lo + 128], T.qu[:], T.su[:], ["t", "u"]) for lo in CH]
+        for b in range(4):
+            d, dn, _ = mm(C, blk(T.qe, b, 128), blk(T.se, b, 128), T.qt[:], T.st[:], ["t", "e%d" % b])
+            a(C, act(blk(T.dp, b, C), d), [], [dn, "dp%d" % b])
+        dma("y", "rep%d" % t, [(T.wd[16 * h:16 * h + 16, :], T.dp[:]) for h in range(8)],
+            ["dp%d" % b for b in range(4)], ["wd"], 11000)
+        for k in range(8):
+            for c in range(3):
+                z = 2 * c + k % 2
+                pm, m = blk(T.pm, z, 64), T.pm[:, 64 * z + 63:64 * z + 64]
+                sa, sb = blk(T.sa, c, 64), blk(T.sb, c, 64)
+                cur = T.ps[:, lik[c][2]:lik[c][2] + 64] if k == 0 else sa
+                cr, cw = ([], [lik[c][1]]) if k == 0 else (["sa%d" % c], [])
+                e, n8 = blk(T.ee, 8 * c + k, 1), blk(T.ng, 8 * c + k, 1)
+                en, nn, pn, fn, cn = "ee%d_%d" % (c, k), "n%d_%d" % (c, k), "pm%d" % z, "fh%d" % z, "cap%d" % c
+                f8 = T.fl[:, 128 * z + 64:128 * z + 72]
+                lt8 = T.lt[:, 64 * c + 7:64 * c + 64:8]
+                v(64, scan(pm, cur, T.neg[:], LOWEST, A.max, A.max), cr + ["neg"], cw + [pn])
+                a(100, act(blk(T.lt, c, 64), pm, F.Sign, bias=m, scale=-1.0, accum_out=e), [pn], ["lt%d" % c, en])
+                a(100, act(lt8, lt8, F.Identity, scale=-8.0, accum_out=n8), [], ["lt%d" % c, nn])
+                if k < 7:
+                    v(64, ts(blk(T.fl, 2 * z, 64), T.gtab[:], n8, None, A.is_equal), ["gtab", nn], ["fg%d" % z])
+                    v(64, ts(blk(T.fl, 2 * z + 1, 64), T.htab[:], e, n8, A.subtract, A.is_equal), ["htab", en, nn], [fn])
+                    v(64, ts(blk(T.cap, c, 128), blk(T.fl, z, 128), -(ALIVE + DEAD), ALIVE, A.mult, A.add), ["fg%d" % z, fn], [cn])
+                    v(64, scan(sb, blk(T.cap, 2 * c, 64), cur, 0.0, A.add, A.min), cr + [cn], cw + ["sb%d" % c])
+                    v(64, scan(sa, blk(T.cap, 2 * c + 1, 64), sb, 0.0, A.add, A.min), [cn, "sb%d" % c], ["sa%d" % c])
+                else:
+                    early[0] = STAGGER * (2 - c)
+                    v(8, ts(f8, T.htab[:, 0:8], e, n8, A.subtract, A.is_equal), ["htab", en, nn], [fn])
+                    early[0] = 0
+                a(8, act(T.sk[:, 64 * c + k:64 * c + 64:8], f8, F.Identity, scale=m), [fn, pn], ["sk%d_%d" % (c, k)])
+                a(8, act(T.gk[:, 64 * c + k:64 * c + 64:8], f8, F.Identity, scale=n8), [fn, nn], ["gk%d_%d" % (c, k)])
+        allk = [(c, k) for c in range(3) for k in range(8)]
+        v(192, scan(T.ss[:, 0:192], T.keep[:], T.sk[:], 0.0, A.mult, A.add), ["keep"] + ["sk%d_%d" % x for x in allk], ["ss"])
+        v(192, scan(T.sg[:], T.keep[:], T.gk[:], 0.0, A.mult, A.add), ["keep"] + ["gk%d_%d" % x for x in allk], ["sg"])
+        ends, ss = (lambda lo, hi: T.ss[lo:hi, 7:256:8]), ["ss", "sspad"]
+        a(32, act(T.zs[:, 0:32], ends(0, 128)), ss, ["zs_0"])
+        zs = spread("a", T.zs, 0, "zs", ends, ss)
+        v(32, tr(T.ta[:, 0:32], ends(0, 128)), ss, ["ta0"])
+        v(32, tr(T.ta[:, 32:64], ends(0, 128)), ss, ["ta1"])
+        v(32, tr(T.zs[:, 128:160], T.ta[:, 16:48]), ["ta0", "ta1"], ["zh_0"])
+        zh = spread("v", T.zs, 128, "zh", (lambda lo, hi: T.zs[lo:hi, 128:160]), ["zh_0"])
+        a(580, act(T.zb[:], T.zs[:, 0:128].indirect(T.off1[:])), zs + ["off1"], ["zb"])
+        v(C, tr(T.row[:], T.zb[:]), ["zb"], ["row"])
+        v(560, cp(T.lb[:], T.zs[:].indirect(T.off2[:])), zs + zh + ["off2"], ["lb"])
+        for c in range(3):
+            v(8, ts(blk(T.zv, c, 8), T.sg[:, 64 * c + 7:64 * c + 64:8], -160.0, blk(T.jcol, c, 1), A.mult, A.add),
+              ["sg", "j0", "j1"], ["zv%d" % c])
+        op(None, 0, None, ["zv0", "zv1", "zv2", "zvpad"], ["zv_0"])
+        zv = spread("a", T.zv, 0, "zv", (lambda lo, hi: T.zv[lo:hi, 0:32]), ["zv_0"])
+        a(580, act(T.zc[:], T.zv[:].indirect(T.off1[:])), zv + ["zv0", "zv1", "zv2", "off1"], ["zc"])
+        v(C, tr(T.val[:], T.zc[:]), ["zc"], ["val"])
+        v(2 * C, tt(T.eq[:], T.row[:], T.lb[:], A.is_equal), ["row", "lb"], ["eq"])
+        v(160, scan(T.cor[:], T.eq[:], T.tri[:], 0.0, A.add, A.mult), ["eq", "tri"], ["cor"])
+        v(40, tt(T.cb[:], T.base[:], T.cor[:, 15:C:16], A.subtract), ["base0", "base1", "cor"], ["cb"])
+        for m in range(20):
+            cut, own = 16 * m + 16, blk(T.lb, 16 * m, 1)
+            if m < NA:
+                o = C * m
+                fore, hind = T.sn[:, o:o + cut], T.sn[:, o + cut:o + C]
+                a(C, act(blk(T.sn, m, C), T.row[:], F.Sign, bias=own, scale=-1.0), ["row", "lb"], ["sna%d" % m, "snb%d" % m])
+                a(cut + 25, act(fore, fore, F.Relu, accum_out=blk(T.a1, m, 1)), [], ["sna%d" % m, "a1_%d" % m])
+                a(C - cut + 25, act(hind, hind, F.Relu, scale=-1.0, accum_out=blk(T.a2, m, 1)), [], ["snb%d" % m, "a2_%d" % m])
+            else:
+                i = m - NA
+                o = C * i
+                v(cut, ts(T.fv[:, o:o + cut], T.row[:, 0:cut], own, 0.5, A.is_ge, A.subtract), ["row", "lb"], ["fva%d" % i])
+                if cut < C:
+                    v(C - cut, ts(T.fv[:, o + cut:o + C], T.row[:, cut:C], own, 0.5, A.is_gt, A.subtract), ["row", "lb"], ["fvb%d" % i])
+                v(80, scan(blk(T.so, i, 160), blk(T.fv, 2 * i, 160), blk(T.fv, 2 * i + 1, 160), 0.0, A.add, A.add),
+                  ["fva%d" % i, "fvb%d" % i], ["so%d" % i])
+        v(16, tt(T.a3[:], T.a2[:], T.a1[:], A.subtract), ["a%d_%d" % (x, m) for x in (1, 2) for m in range(NA)], ["a3"])
+        v(16, tt(T.rk[:, 0:NA], T.a3[:], T.cb[:, 0:NA], A.add), ["a3", "cb"], ["rka"])
+        v(24, tt(T.rk[:, NA:20], T.so[:, 159:160 * NV:160], T.cb[:, NA:20], A.add), ["cb"] + ["so%d" % i for i in range(NV)], ["rkv"])
+        v(20, cp(T.offr[:], T.rk[:]), ["rka", "rkv"], ["offr"])
+        v(1250, cp(T.wo[:].indirect(T.offr[:]), T.val[:]), ["offr", "val"], ["wo"])
+        v(C, tr(T.tt[:, 0:C], T.wo[:, 0:C]), ["wo"], ["tt0"])
+        v(C, tr(T.tt[:, C:2 * C], T.wo[:, 16:16 + C]), ["wo"], ["tt1"])
+        v(110, cp(T.offb[:], T.tt[:].indirect(T.off3[:])), ["tt0", "tt1", "off3"], ["offb"])
+        for b in range(4):
+            put, mk = (v, cp) if b < 2 else (a, act)
+            put(570, mk(T.bt[:, b:4 * C:4], T.wd[:, C * b:32 * C].indirect(T.offb[:, 0:20])), ["wd", "offb"], ["bt%d" % b])
+        qb, sq, qm, sm = T["qb%d" % t], T["sq%d" % t], T["qm%d" % t], T["sm%d" % t]
+        quant(qb[:], sq[:], T.bt[:], C, ["bt%d" % b for b in range(4)], ["qb%d" % t])
+
+        def deal(t=t, qb=qb, sq=sq, qm=qm, sm=sm):
+            for kind in (0, 1):
+                tf = []
+                for d in range(1, N):
+                    j = (rank + d) % N
+                    rid, pid = topo.addr(T.cores[j], core)
+                    eng = topo.engines(core, T.cores[j])
+                    src, dst = (u8(blk(qb, j, L)), u8(blk(qm, rank, L))) if kind == 0 else (blk(sq, j, L), blk(sm, rank, L))
+                    tf.append(RemoteDMATransfer(dst_ids=[DstId(rid=rid, pnc=pid)], dma_engine_mask=1 << eng[d - 1 + kind],
+                                                remote_sem=T.sem["arr%d" % t], src=src, dst=dst))
+                g.remote_dma_fused(tf, local_sem=T.sem["snd%d" % t])
+        sent = op("g", 1500, deal, ["qb%d" % t], [], sem="snd%d" % t, inc=2 * (N - 1), lat=6000)
+        op(None, 0, None, [], ["marr%d" % t], sem="arr%d" % t, inc=2 * (N - 1), after=[sent])
+        dma("y", "own%d" % t, [(u8(blk(qm, rank, L)), u8(blk(qb, rank, L))), (blk(sm, rank, L), blk(sq, rank, L))],
+            ["qb%d" % t], ["mown%d" % t], 2400)
+        if t == ROUNDS - 1:
+            v(336, ts(T.t1[:], T.wo[:, 0:336], 1.0 / 1280, None, A.mult), ["wo", "qb%d" % t], ["t1"])
+            v(336, cp(T.t2[:], T.t1[:]), ["t1"], ["t2"])
+            v(336, ts(T.t3[:], T.t2[:], -1280.0, None, A.mult), ["t2"], ["t3"])
+            v(672, tt(T.oo[:], T.t3[:], T.wo[:, 0:336], A.add), ["t3", "wo"], ["oo"])
+            v(C, ts(T.g1[:], T.val[:], 1.0 / 1280, None, A.mult), ["val", "qb%d" % t], ["g1"])
+            v(C, cp(T.g2[:], T.g1[:]), ["g1"], ["g2"])
+            v(C, cp(T.g3[:], T.g2[:]), ["g2"], ["g3"])
+            dma("y", "ol1", [(T.ol[0:8:2, 0:C], T.oo[0:128:32, 0:C]), (T.ol[1:8:2, 0:C], T.oo[16:128:32, 16:16 + C])], ["oo"], [], 2400)
+            dma("y", "ol2", [(T.ol[:, C:2 * C], T.g3[0:128:16, :])], ["g3"], [], 2400)
+        got = ["marr%d" % t, "mown%d" % t]
+        for b in range(4):
+            w, wn, _ = mm(C, blk(T.qw, b, 128), blk(T.sw, b, 128), qm[:], sm[:], got + ["w"])
+            d, dn, _ = mm(C, blk(T.qe, 4 + b, 128), blk(T.se, 4 + b, 128), qm[:], sm[:], got + ["e%d" % (4 + b)])
+            a(C, act(blk(T.rr, b, C), w, F.Relu, scale=0.03125), [], [wn, "rr%d" % b])
+            v(C, tt(T.xs[:, b:4 * C:4], d, blk(T.rr, b, C), A.add), ["rr%d" % b], [dn, "xs%d" % b])
+        quant(T.qt[:], T.st[:], T.xs[:], C, ["xs%d" % b for b in range(4)], ["t"])
+
+    d, dn, _ = mm(C, T.qv[:], T.sv[:], T.qt[:], T.st[:], ["t", "v"])
+    v(C, cp(T.yo[:], d), [], [dn, "yo"])
+    dma("y", "oy", [(T.y[:], T.yo[:])], ["yo"], [], 2400)
+    dma("a", "oq", [(T.oc[:], u8(T.qt[:]))] + [(T.osc[4 * k:4 * k + 4, :], T.st[32 * k:32 * k + 4, :]) for k in range(4)],
+        ["t"], [], 2400)
+
+    n = len(ops)
+    succ = [[] for _ in range(n)]
+    for i, o in enumerate(ops):
+        for d in o["deps"] | o["soft"]:
+            succ[d].append(i)
+    ahead = [0.0] * n
+    for i in range(n - 1, -1, -1):
+        ahead[i] = ops[i]["cost"] + ops[i]["lat"] + ops[i]["early"] + max([ahead[j] + HOP_CROSS for j in succ[i]], default=0)
+    left = [len(o["deps"] | o["soft"]) for o in ops]
+    ready_at, free, order = [0.0] * n, {k: 0.0 for k in queue}, []
+    ready = [i for i in range(n) if left[i] == 0]
+    while ready:
+        start = {i: max(ready_at[i], free.get(ops[i]["eng"], 0.0)) for i in ready}
+        first = min(ready, key=lambda i: start[i])
+        near = [i for i in ready if ops[i]["eng"] == ops[first]["eng"] and start[i] <= start[first] + 40]
+        i = max(near, key=lambda i: ahead[i])
+        ready.remove(i)
+        order.append(i)
+        o = ops[i]
+        end = start[i] + o["cost"]
+        if o["eng"] is not None:
+            free[o["eng"]] = end
+        for j in succ[i]:
+            hop = 0 if o["eng"] is None or i not in ops[j]["deps"] else (HOP_SAME if ops[j]["eng"] == o["eng"] else HOP_CROSS)
+            ready_at[j] = max(ready_at[j], end + o["lat"] + hop)
+            left[j] -= 1
+            if left[j] == 0:
+                ready.append(j)
+
+    count = {k: 0 for k in SEMAPHORES}
+    known = {k: {} for k in queue}
+    need = [None] * n
+    for i in order:
+        o = ops[i]
+        if o["eng"] is None:
+            if o["sem"] is not None:
+                count[o["sem"]] += o["inc"]
+                need[i] = [(o["sem"], count[o["sem"]], {})]
+            else:
+                need[i] = [x for d in o["deps"] for x in need[d]]
+            continue
+        kn = known[o["eng"]]
+        wants = sorted([x for d in o["deps"] for x in need[d]], key=lambda x: -len(x[2]) * 100000 - x[1])
+        if o["eng"] == "g" and o["sem"] is None:
+            wants.append(("cg", count["cg"], {}))
+        for s, c, snap in wants:
+            if kn.get(s, 0) < c:
+                kn[s] = max(c2 for s2, c2, _ in wants if s2 == s)
+                queue[o["eng"]].wait_ge(T.sem[s], kn[s])
+            for s2, c2 in snap.items():
+                kn[s2] = max(kn.get(s2, 0), c2)
+        if o["sem"] is None:
+            s = "c" + o["eng"]
+            o["fn"]().then_inc(T.sem[s], 1)
+            count[s] += 1
+        else:
+            s = o["sem"]
+            o["fn"]()
+            count[s] += o["inc"]
+        need[i] = [(s, count[s], dict(kn))]
+    for s in SEMAPHORES:
+        if count[s]:
+            g.wait_ge(T.sem[s], count[s])

@@ -4,12 +4,12 @@ from concourse.mybir import dt, AluOpType, ActivationFunctionType
 C, L, ROUNDS, N = 320, 40, 3, 8
 NA = 8
 NV = 20 - NA
-ALIVE, DEAD, LOWEST = 2.0 ** 90, 2.0 ** 80, -(2.0 ** 95)
+DEAD, GONE, LOWEST = 2.0 ** 80, 2.0 ** 90, -(2.0 ** 95)
 _B = {
     "bfloat16": dict(x0=4 * C, ut=512, vt=512, xs=4 * C, ones=512, et=4096, dp=4 * C, wd=32 * C, bt=4 * C, htab=64, gtab=64,
-                     tri=C, lt=192, fl=768, cap=384, eq=C, cor=C, fv=NV * C, so=NV * 160, sn=NA * C),
+                     tri=C, lt=192, lg=24, fl=768, fe=48, eq=C, cor=C, fv=NV * C, so=NV * 160, sn=NA * C),
     "float32": dict(rr=4 * C, neg=64, keep=192, pf=16, jcol=4, o1i=20, utab=20, o2f=20, o3f=2, base=20, pm=384, ee=24, ng=24,
-                    sa=192, sb=192, sk=192, gk=192, ss=256, sg=192, ta=64, zs=256, zv=128, zb=C, row=C, lb=C, zc=C, val=C,
+                    hh=24, sa=192, sb=192, sk=192, gk=192, ss=256, sg=192, ta=64, zs=256, zv=128, zb=C, row=C, lb=C, zc=C, val=C,
                     cb=20, a1=NA, a2=NA, a3=NA, rk=20, wo=352, tt=2 * C, t1=336, t3=336, oo=336, g1=C, g3=C, yo=C),
     "int32": dict(pi=8, t2=336, g2=C),
     "uint16": dict(off1=20, off2=20, off3=2, offr=20, offb=32),
@@ -23,9 +23,17 @@ SEMAPHORES = (["cv", "ca", "cp", "cg", "lx", "lu1", "lu2", "lw", "lv", "ol1", "o
 
 A = AluOpType
 F = ActivationFunctionType
-HOP_SAME, HOP_CROSS = 70, 110
+HOP_SAME, HOP_CROSS = 200, 200
 STAGGER = 400
 CH = (0, 128, 192)
+
+
+def u8(view):
+    return view.bitcast(dt.uint8)
+
+
+def blk(buf, k, n):
+    return buf[:, n * k:n * k + n]
 
 
 def rank_program(g, core, T, topo):
@@ -98,12 +106,6 @@ def rank_program(g, core, T, topo):
     def fiota(out, pat, base, cm, n, w):
         iota(out, pat, base, cm, n, w, allow_small_or_imprecise_dtypes=True)
 
-    def u8(view):
-        return view.bitcast(dt.uint8)
-
-    def blk(buf, k, n):
-        return buf[:, n * k:n * k + n]
-
     dma("y", "lx", [(T.x0[:], T.x[:])], [], ["x0"], 3200)
     uc = [(blk(T.ut, k, 32), T.u[:, 64 * k:64 * k + 32]) for k in range(8)]
     dma("a", "lu1", uc[:5], [], ["ut1"], 2600)
@@ -114,8 +116,8 @@ def rank_program(g, core, T, topo):
     quant(T.qu[:], T.su[:], T.ut[:], 128, ["ut1", "ut2"], ["u"])
     quant(T.qv[:], T.sv[:], T.vt[:], 128, ["vt"], ["v"])
 
-    fiota(T.htab[:], [[0, 8], [1, 8]], 0, 0, 64, ["htab"])
-    fiota(T.gtab[:], [[-8, 8], [0, 8]], 0, 0, 64, ["gtab"])
+    fiota(T.htab[:], [[0, 8], [8, 8]], 0, 0, 64, ["htab"])
+    fiota(T.gtab[:], [[1, 8], [0, 8]], 0, 0, 64, ["gtab"])
     v(64, fill(T.neg[:], LOWEST), [], ["neg"])
     v(256, fill(T.ones[:], 1.0), [], ["ones"])
     for e in range(8):
@@ -124,7 +126,7 @@ def rank_program(g, core, T, topo):
            ["ones"], ["et%d" % e])
         quant(blk(T.qe, e, 128), blk(T.se, e, 128), blk(T.et, e, 512), 128, ["et%d" % e], ["e%d" % e])
     fiota(T.keep[:], [[0, 24], [1, 8]], 0, 0, 192, ["keep"])
-    v(192, ts(T.keep[:], T.keep[:], 0.0, None, A.is_gt), ["keep"], ["keep"])
+    v(192, ts(T.keep[:], T.keep[:], 0.0, LOWEST, A.is_equal, A.mult), ["keep"], ["keep"])
     iota(T.pi[:, 0:1], [[0, 1]], 0, 1, 1, ["pi0"])
     v(1, ts(T.pi[:, 1:2], T.pi[:, 0:1], 1, None, A.bitwise_and), ["pi0"], ["pi1"])
     v(1, ts(T.pi[:, 2:3], T.pi[:, 0:1], 15, None, A.bitwise_and), ["pi0"], ["pi2"])
@@ -181,7 +183,7 @@ def rank_program(g, core, T, topo):
             d, dn, _ = mm(C, blk(T.qe, b, 128), blk(T.se, b, 128), T.qt[:], T.st[:], ["t", "e%d" % b])
             a(C, act(blk(T.dp, b, C), d), [], [dn, "dp%d" % b])
         dma("y", "rep%d" % t, [(T.wd[16 * h:16 * h + 16, :], T.dp[:]) for h in range(8)],
-            ["dp%d" % b for b in range(4)], ["wd"], 11000)
+            ["dp%d" % b for b in range(4)], ["wd"], 22000)
         for k in range(8):
             for c in range(3):
                 z = 2 * c + k % 2
@@ -189,28 +191,28 @@ def rank_program(g, core, T, topo):
                 sa, sb = blk(T.sa, c, 64), blk(T.sb, c, 64)
                 cur = T.ps[:, lik[c][2]:lik[c][2] + 64] if k == 0 else sa
                 cr, cw = ([], [lik[c][1]]) if k == 0 else (["sa%d" % c], [])
-                e, n8 = blk(T.ee, 8 * c + k, 1), blk(T.ng, 8 * c + k, 1)
-                en, nn, pn, fn, cn = "ee%d_%d" % (c, k), "n%d_%d" % (c, k), "pm%d" % z, "fh%d" % z, "cap%d" % c
-                f8 = T.fl[:, 128 * z + 64:128 * z + 72]
-                lt8 = T.lt[:, 64 * c + 7:64 * c + 64:8]
+                e, ge, h8 = blk(T.ee, 8 * c + k, 1), blk(T.ng, 8 * c + k, 1), blk(T.hh, 8 * c + k, 1)
+                en, nn, hn, pn, fn = "ee%d_%d" % (c, k), "n%d_%d" % (c, k), "h%d_%d" % (c, k), "pm%d" % z, "fe%d" % z
+                f8, lt8 = blk(T.fe, z, 8), T.lt[:, 64 * c + 7:64 * c + 64:8]
                 v(64, scan(pm, cur, T.neg[:], LOWEST, A.max, A.max), cr + ["neg"], cw + [pn])
                 a(100, act(blk(T.lt, c, 64), pm, F.Sign, bias=m, scale=-1.0, accum_out=e), [pn], ["lt%d" % c, en])
-                a(100, act(lt8, lt8, F.Identity, scale=-8.0, accum_out=n8), [], ["lt%d" % c, nn])
+                a(100, act(lt8, lt8, F.Identity, scale=-64.0, bias=e, accum_out=h8), [en], ["lt%d" % c, hn])
+                a(100, act(blk(T.lg, c, 8), T.pm[:, 64 * z + 7:64 * z + 64:8], F.Sign, bias=m, scale=-1.0, accum_out=ge),
+                  [pn], ["lg%d" % c, nn])
                 if k < 7:
-                    v(64, ts(blk(T.fl, 2 * z, 64), T.gtab[:], n8, None, A.is_equal), ["gtab", nn], ["fg%d" % z])
-                    v(64, ts(blk(T.fl, 2 * z + 1, 64), T.htab[:], e, n8, A.subtract, A.is_equal), ["htab", en, nn], [fn])
-                    v(64, ts(blk(T.cap, c, 128), blk(T.fl, z, 128), -(ALIVE + DEAD), ALIVE, A.mult, A.add), ["fg%d" % z, fn], [cn])
-                    v(64, scan(sb, blk(T.cap, 2 * c, 64), cur, 0.0, A.add, A.min), cr + [cn], cw + ["sb%d" % c])
-                    v(64, scan(sa, blk(T.cap, 2 * c + 1, 64), sb, 0.0, A.add, A.min), [cn, "sb%d" % c], ["sa%d" % c])
+                    v(64, ts(blk(T.fl, 2 * z, 64), T.gtab[:], ge, -DEAD, A.is_equal, A.mult), ["gtab", nn], ["fg%d" % z])
+                    v(64, ts(blk(T.fl, 2 * z + 1, 64), T.htab[:], h8, -DEAD, A.is_equal, A.mult), ["htab", hn], ["fh%d" % z])
+                    v(128 if k else 64, tt(sb, cur, blk(T.fl, 2 * z, 64), A.add), cr + ["fg%d" % z], cw + ["sb%d" % c])
+                    v(128, tt(sa, sb, blk(T.fl, 2 * z + 1, 64), A.add), ["fh%d" % z, "sb%d" % c], ["sa%d" % c])
                 else:
                     early[0] = STAGGER * (2 - c)
-                    v(8, ts(f8, T.htab[:, 0:8], e, n8, A.subtract, A.is_equal), ["htab", en, nn], [fn])
-                    early[0] = 0
-                a(8, act(T.sk[:, 64 * c + k:64 * c + 64:8], f8, F.Identity, scale=m), [fn, pn], ["sk%d_%d" % (c, k)])
-                a(8, act(T.gk[:, 64 * c + k:64 * c + 64:8], f8, F.Identity, scale=n8), [fn, nn], ["gk%d_%d" % (c, k)])
+                v(8, ts(f8, T.htab[:, 0:8], h8, None, A.not_equal), ["htab", hn], [fn])
+                early[0] = 0
+                a(8, act(T.sk[:, 64 * c + k:64 * c + 64:8], f8, F.Identity, scale=-GONE, bias=m), [fn, pn], ["sk%d_%d" % (c, k)])
+                a(8, act(T.gk[:, 64 * c + k:64 * c + 64:8], f8, F.Identity, scale=-GONE, bias=ge), [fn, nn], ["gk%d_%d" % (c, k)])
         allk = [(c, k) for c in range(3) for k in range(8)]
-        v(192, scan(T.ss[:, 0:192], T.keep[:], T.sk[:], 0.0, A.mult, A.add), ["keep"] + ["sk%d_%d" % x for x in allk], ["ss"])
-        v(192, scan(T.sg[:], T.keep[:], T.gk[:], 0.0, A.mult, A.add), ["keep"] + ["gk%d_%d" % x for x in allk], ["sg"])
+        v(192, scan(T.ss[:, 0:192], T.keep[:], T.sk[:], LOWEST, A.add, A.max), ["keep"] + ["sk%d_%d" % x for x in allk], ["ss"])
+        v(192, scan(T.sg[:], T.keep[:], T.gk[:], LOWEST, A.add, A.max), ["keep"] + ["gk%d_%d" % x for x in allk], ["sg"])
         ends, ss = (lambda lo, hi: T.ss[lo:hi, 7:256:8]), ["ss", "sspad"]
         a(32, act(T.zs[:, 0:32], ends(0, 128)), ss, ["zs_0"])
         zs = spread("a", T.zs, 0, "zs", ends, ss)
@@ -222,7 +224,7 @@ def rank_program(g, core, T, topo):
         v(C, tr(T.row[:], T.zb[:]), ["zb"], ["row"])
         v(560, cp(T.lb[:], T.zs[:].indirect(T.off2[:])), zs + zh + ["off2"], ["lb"])
         for c in range(3):
-            v(8, ts(blk(T.zv, c, 8), T.sg[:, 64 * c + 7:64 * c + 64:8], -160.0, blk(T.jcol, c, 1), A.mult, A.add),
+            v(8, ts(blk(T.zv, c, 8), T.sg[:, 64 * c + 7:64 * c + 64:8], 1280.0, blk(T.jcol, c, 1), A.mult, A.add),
               ["sg", "j0", "j1"], ["zv%d" % c])
         op(None, 0, None, ["zv0", "zv1", "zv2", "zvpad"], ["zv_0"])
         zv = spread("a", T.zv, 0, "zv", (lambda lo, hi: T.zv[lo:hi, 0:32]), ["zv_0"])

@@ -2,30 +2,39 @@ from concourse.bass import DstId, RemoteDMATransfer
 from concourse.mybir import dt, AluOpType, ActivationFunctionType
 
 C, L, ROUNDS, N = 320, 40, 3, 8
-NA = 8
-NV = 20 - NA
-DEAD, GONE, LOWEST = 2.0 ** 80, 2.0 ** 90, -(2.0 ** 95)
+CH = (0, 64, 192)
+PIECES = ((0, 192), (192, C))
+BANKS = ((3, 4, 5, 6, 7, 0, 1, 2), (3, 4, 5, 6, 7, 2, 3, 4))
+NV = 13
+WIDE = (320, 256, 192, 128, 128)
+AT = [sum(WIDE[:k]) for k in range(5)]
+LANE = {m: ((20 - m) // 4, m % 4) for m in range(1, 20)}
+LANE[0] = (0, 0)
+ORDER = (0, 4, 3, 2, 1)
+HELP = True
+DEAD, STEP, GONE, LOWEST = 2.0 ** 98, 2.0 ** 94, 2.0 ** 90, -(2.0 ** 95)
+LIFT, DROP, WHOLE = 32768.0, 20480.0, 1.5 * 2 ** 23
 _B = {
-    "bfloat16": dict(x0=4 * C, ut=512, vt=512, xs=4 * C, ones=512, et=4096, dp=4 * C, wd=32 * C, bt=4 * C, htab=64, gtab=64,
-                     tri=C, lt=192, lg=24, fl=768, fe=48, eq=C, cor=C, fv=NV * C, so=NV * 160, sn=NA * C),
-    "float32": dict(rr=4 * C, neg=64, keep=192, pf=16, jcol=4, o1i=20, utab=20, o2f=20, o3f=2, base=20, pm=384, ee=24, ng=24,
-                    hh=24, sa=192, sb=192, sk=192, gk=192, ss=256, sg=192, ta=64, zs=256, zv=128, zb=C, row=C, lb=C, zc=C, val=C,
-                    cb=20, a1=NA, a2=NA, a3=NA, rk=20, wo=352, tt=2 * C, t1=336, t3=336, oo=336, g1=C, g3=C, yo=C),
-    "int32": dict(pi=8, t2=336, g2=C),
-    "uint16": dict(off1=20, off2=20, off3=2, offr=20, offb=32),
-    "float8_e4m3fn_x4": dict(qu=128, qv=128, qw=512, qt=C, qe=1024, qb0=C, qb1=C, qb2=C, qm0=C, qm1=C, qm2=C),
-    "uint8": dict(su=128, sv=128, sw=512, st=C, se=1024, sq0=C, sq1=C, sq2=C, sm0=C, sm1=C, sm2=C),
+    "bfloat16": dict(x0=4 * C, ut=512, vt=512, xs=4 * C, ones=516, et=516, wd=32 * C, bt=4 * C, htab=64, gtab=64, t16=C + 16, kc=C + 16, kd=C,
+                     tri=C, lt=192, lg=24, fl=768, pen=192, eq=C, cor=C, k16=C, og=512, ft=4096, so=16 * 160, sn=12 * C),
+    "float32": dict(rr=4 * C, neg=64, keep=64, vtab=256, pf=24, o1i=20, utab=20, o2f=32, o3f=32, o4f=2, of=8, base=20,
+                    pm=384, ee=24, ng=24, hh=24, sa=192, sb=192, ab=192, sk=192, sv=384, ta=240, zs=416, zb=C, row=C, ow=32,
+                    zc=C, val=C, kr=C, dr=C, cb=20, a1=20, wo=C, dg=C, t1=C, t3=C, oo=C, g1=C, g2=C, g3=C, yo=C),
+    "int32": dict(pi=8),
+    "uint16": dict(off1=20, off2=20, offo=2, offu=8, offp=4, offr=20, offb=20),
+    "float8_e4m3fn_x4": dict(qu0=128, qu=128, qv=128, qw=512, qt=C, qe=512, qf=1024, qo=128, qb0=C, qb1=C, qb2=C, qm0=C, qm1=C, qm2=C),
+    "uint8": dict(su0=128, su=128, sv8=128, sw=512, st=C, se=512, sf=1024, so8=128, sq0=C, sq1=C, sq2=C, sm0=C, sm1=C, sm2=C,
+                  hl0=4 * L, hl1=4 * L, hl2=4 * L),
 }
 SCRATCH = {k: ("sbuf", [128, n], d) for d, bufs in _B.items() for k, n in bufs.items()}
 SCRATCH["ps"] = ("psum", [128, 4096], "float32")
-SEMAPHORES = (["cv", "ca", "cp", "cg", "lx", "lu1", "lu2", "lw", "lv", "ol1", "ol2", "oy", "oq"]
-              + ["%s%d" % (a, t) for a in ("rep", "own", "snd", "arr") for t in range(ROUNDS)])
+SEMAPHORES = (["cv", "ca", "cp", "cg", "lx", "lu", "lw", "lv", "ol1", "ol2", "oy", "oq", "hout"]
+              + ["%s%d" % (a, t) for a in ("rep", "own", "snd", "arr", "hin") for t in range(ROUNDS)])
 
 A = AluOpType
 F = ActivationFunctionType
-HOP_SAME, HOP_CROSS = 200, 200
-STAGGER = 400
-CH = (0, 128, 192)
+HOP, NEAR, STAGGER = 180, 100, 400
+TURNS = [(0, 0), (0, 0), (0, 2), (0, 1), (1, 1), (1, 3), (1, 4), (2, 2)]
 
 
 def u8(view):
@@ -36,13 +45,35 @@ def blk(buf, k, n):
     return buf[:, n * k:n * k + n]
 
 
+def transfer(topo, core, to, engines, sem, src, dst):
+    rid, pid = topo.addr(to, core)
+    return RemoteDMATransfer(dst_ids=[DstId(rid=rid, pnc=pid)], dma_engine_mask=sum(1 << e for e in engines), remote_sem=sem, src=src, dst=dst)
+
+
+def helpers(core, T, topo):
+    free = [c for c in topo.cores_of(core) if T.rank_of(c) is None]
+    return sorted(free, key=lambda c: topo.die(c) != topo.die(core))[:2]
+
+
+def helper_program(g, core, T, topo, rank, half):
+    to = [j for j in range(4 * half, 4 * half + 4) if j != rank]
+    for t in range(ROUNDS):
+        g.wait_ge(T.sem["hin%d" % t], 4)
+        g.remote_dma_fused([transfer(topo, core, T.cores[j], topo.engines(core, T.cores[j])[2 * (j % 4):2 * (j % 4) + 2], T.sem["arr%d" % t],
+                                     blk(T["hl%d" % t], j % 4, L), blk(T["sm%d" % t], rank, L)) for j in to], local_sem=T.sem.hout)
+    g.wait_ge(T.sem.hout, 2 * len(to) * ROUNDS)
+
+
 def rank_program(g, core, T, topo):
     rank = T.rank_of(core)
     if rank is None:
+        for r, c in enumerate(T.cores):
+            if HELP and core in helpers(c, T, topo):
+                helper_program(g, core, T, topo, r, helpers(c, T, topo).index(core))
         return
     V, S, P, Y = g.vector, g.scalar, g.tensor, g.sync
     queue = {"v": V, "a": S, "p": P, "g": g, "y": Y}
-    ops, writer, readers, early, mms = [], {}, {}, [0], []
+    ops, writer, readers, early, mms, gs = [], {}, {}, [0], [], []
 
     def op(eng, cost, fn, r=(), w=(), sem=None, inc=0, lat=0, after=(), soft=()):
         deps = set(after) | {writer[k] for k in list(r) + list(w) if k in writer}
@@ -59,10 +90,10 @@ def rank_program(g, core, T, topo):
         return i
 
     def v(n, fn, r, w):
-        return op("v", max(64, n) + 8, fn, r, w)
+        return op("v", max(64, n) + 10, fn, r, w)
 
     def a(n, fn, r, w):
-        return op("a", max(78, n) + 8, fn, r, w)
+        return op("a", max(64, n) + 40, fn, r, w)
 
     def dma(eng, sem, pairs, r, w, lat):
         def fn():
@@ -70,14 +101,16 @@ def rank_program(g, core, T, topo):
                 queue[eng].dma_start(o, i).then_inc(T.sem[sem], 16)
         return op(eng, 100 * len(pairs), fn, r, w, sem=sem, inc=16 * len(pairs), lat=lat)
 
-    def mm(n, lq, ls, rq, rs, r):
-        bank = len(mms) % 8
-        out = T.ps[:, 512 * bank:512 * bank + n]
-        mms.append(op("p", 1.3 * n + 60, lambda: P.matmul_mx(out, lq, ls, rq, rs, True, True), r, ["b%d" % bank], soft=mms[-1:]))
-        return out, "b%d" % bank, 512 * bank
+    def mm(lq, ls, rq, rs, r, bank=None, start=True, stop=True):
+        n = rq.shape[1]
+        bank = 3 + len(mms) % 5 if bank is None else bank
+        out, name = T.ps[:, 512 * bank:512 * bank + n], "b%d" % bank
+        mms.append(op("p", 1.3 * n + 60, lambda: P.matmul_mx(out, lq, ls, rq, rs, start, stop), r, [name] if start else [], soft=mms[-1:]))
+        writer[name] = mms[-1]
+        return out, name
 
-    def quant(q, s, src, n, r, w):
-        op("v", 20 + 1.1 * n, lambda: V.quantize_mx(q, s, src), r, w)
+    def quant(q, s, src, r, w):
+        return op("v", 20 + 1.1 * q.shape[1], lambda: V.quantize_mx(q, s, src), r, w)
 
     def ts(out, in0, s1, s2, *o):
         return lambda: V.tensor_scalar(out, in0, s1, s2, *o)
@@ -100,207 +133,239 @@ def rank_program(g, core, T, topo):
     def fill(out, x):
         return lambda: V.memset(out, x)
 
-    def iota(out, pat, base, cm, n, w, **kw):
-        op("g", 160 + 2 * n, lambda: g.iota(out, pat, base, cm, **kw), [], w)
+    def move(eng, n, out, in_, r, w):
+        return v(n, cp(out, in_), r, w) if eng == "v" else a(n, act(out, in_), r, w)
 
-    def fiota(out, pat, base, cm, n, w):
-        iota(out, pat, base, cm, n, w, allow_small_or_imprecise_dtypes=True)
+    def lin(n, out, in_, scale, bias, r, w):
+        a(n, act(out, in_, F.Identity, scale=scale, bias=bias), r, w)
+
+    def iota(out, pat, base, cm, n, w, wait=False, **kw):
+        gs.append(op("g", 160 + 2 * n, lambda: g.iota(out, pat, base, cm, **kw), [], w, soft=gs[-1:], after=gs[-1:] if wait else []))
+
+    def fiota(out, pat, base, cm, n, w, wait=False):
+        iota(out, pat, base, cm, n, w, wait, allow_small_or_imprecise_dtypes=True)
 
     dma("y", "lx", [(T.x0[:], T.x[:])], [], ["x0"], 3200)
-    uc = [(blk(T.ut, k, 32), T.u[:, 64 * k:64 * k + 32]) for k in range(8)]
-    dma("a", "lu1", uc[:5], [], ["ut1"], 2600)
-    dma("y", "lu2", uc[5:] + [(T.ut[:, 256:512], T.u[:, 0:256])], [], ["ut2"], 2600)
-    dma("y", "lw", [(u8(T.qw[:]), T.wc[:]), (T.sw[:], T.ws[:])], [], ["w"], 3000)
-    dma("y", "lv", [(T.vt[:], T.v[:])], [], ["vt"], 2600)
-    quant(T.qt[:], T.st[:], T.x0[:], C, ["x0"], ["t"])
-    quant(T.qu[:], T.su[:], T.ut[:], 128, ["ut1", "ut2"], ["u"])
-    quant(T.qv[:], T.sv[:], T.vt[:], 128, ["vt"], ["v"])
+    dma("a", "lu", [(T.ut[:], T.u[:])], [], ["ut"], 2600)
+    dma("y", "lw", [(u8(T.qw[:]), T.wc[:]), (T.sw[:], T.ws[:])], [], ["w"], 9000)
+    dma("y", "lv", [(T.vt[:], T.v[:])], [], ["vt"], 30000)
+    quant(T.qt[:], T.st[:], T.x0[:], ["x0"], ["t0", "t1"])
+    quant(T.qu0[:], T.su0[:], T.ut[:], ["ut"], ["u0"])
+    quant(T.qv[:], T.sv8[:], T.vt[:], ["vt"], ["v"])
 
+    iota(T.pi[:, 0:1], [[0, 1]], 0, 1, 1, ["pi0"])
+    fiota(T.t16[:], [[0, 21], [1, 16]], 0, 0, C + 16, ["t16"])
+    v(258, fill(T.ones[:], 1.0), [], ["ones"])
+    gs.append(op("g", 1240, lambda: g.affine_select(T.et[:], T.ones[:], [[1, 516]], A.is_equal, 0.0, -3, -4), ["ones"], ["et"], soft=gs[-1:]))
+    for b in range(4):
+        quant(blk(T.qe, b, 128), blk(T.se, b, 128), T.et[:, 3 - b:515 - b], ["et"], ["e%d" % b])
+
+    def unpack(b, q, s, rs, bank=None):
+        return mm(blk(T.qe, b, 128), blk(T.se, b, 128), q, s, rs + ["e%d" % b], bank)
     fiota(T.htab[:], [[0, 8], [8, 8]], 0, 0, 64, ["htab"])
     fiota(T.gtab[:], [[1, 8], [0, 8]], 0, 0, 64, ["gtab"])
+    for k, (sh, mask) in enumerate([(0, 15), (4, 1), (3, 1), (0, 7), (4, 7)]):
+        v(1, ts(blk(T.pi, k + 1, 1), T.pi[:, 0:1], sh, mask, A.logical_shift_right, A.bitwise_and), ["pi0"], ["pi%d" % (k + 1)])
+    v(6, cp(T.pf[:, 16:22], T.pi[:, 0:6]), ["pi%d" % k for k in range(6)], ["pf"])
+    pp, pl, ph, p8, p7, pg = [blk(T.pf, k, 1) for k in range(16, 22)]
+    c4, c8 = T.t16[:, 0:4], T.t16[:, 0:8]
+
+    def col(k, in_, scale, bias, r=()):
+        lin(1, blk(T.pf, k, 1), in_, scale, bias, ["pf"] + list(r), ["pf%d" % k])
+        return blk(T.pf, k, 1)
+    v(4, ts(T.offu[:, 0:4], c4, 32.0, col(5, p8, 16.0, p7), A.mult, A.add), ["t16", "pf5"], ["offu0"])
+    v(4, ts(T.offu[:, 4:8], c4, 2.0, col(6, p7, 16.0, p8), A.mult, A.add), ["t16", "pf6"], ["offu1"])
+    v(4, ts(T.offp[:], c4, 2.0, col(7, p7, 8.0, p8), A.mult, A.add), ["t16", "pf7"], ["offp"])
+    v(250, cp(T.qu[:].bitcast(dt.uint32), T.qu0[:].bitcast(dt.uint32).indirect(T.offu[:])), ["u0", "offu0", "offu1"], ["uq"])
+    a(250, act(T.su[:], T.su0[:].indirect(T.offu[:])), ["u0", "offu0", "offu1"], ["us"])
     v(64, fill(T.neg[:], LOWEST), [], ["neg"])
-    v(256, fill(T.ones[:], 1.0), [], ["ones"])
-    for e in range(8):
-        pat = [[4, 16], [64, 8], [1, 4]] if e < 4 else [[1, 512]]
-        op("g", 1224, (lambda e=e, pat=pat: g.affine_select(blk(T.et, e, 512), T.ones[:], pat, A.is_equal, 0.0, -(e % 4), -4)),
-           ["ones"], ["et%d" % e])
-        quant(blk(T.qe, e, 128), blk(T.se, e, 128), blk(T.et, e, 512), 128, ["et%d" % e], ["e%d" % e])
-    fiota(T.keep[:], [[0, 24], [1, 8]], 0, 0, 192, ["keep"])
-    v(192, ts(T.keep[:], T.keep[:], 0.0, LOWEST, A.is_equal, A.mult), ["keep"], ["keep"])
-    iota(T.pi[:, 0:1], [[0, 1]], 0, 1, 1, ["pi0"])
-    v(1, ts(T.pi[:, 1:2], T.pi[:, 0:1], 1, None, A.bitwise_and), ["pi0"], ["pi1"])
-    v(1, ts(T.pi[:, 2:3], T.pi[:, 0:1], 15, None, A.bitwise_and), ["pi0"], ["pi2"])
-    v(1, ts(T.pi[:, 3:4], T.pi[:, 0:1], 4, 1, A.logical_shift_right, A.bitwise_and), ["pi0"], ["pi3"])
-    v(4, cp(T.pf[:, 0:4], T.pi[:, 0:4]), ["pi0", "pi1", "pi2", "pi3"], ["pf"])
-    pu, pl, ph = T.pf[:, 1:2], T.pf[:, 2:3], T.pf[:, 3:4]
-    v(1, ts(T.pf[:, 4:5], ph, -256.0, 127.0, A.mult, A.add), ["pf"], ["pf4"])
-    v(1, ts(T.pf[:, 5:6], ph, 129.0, None, A.mult), ["pf"], ["pf5"])
-    v(1, ts(T.pf[:, 6:7], ph, 16.0, None, A.mult), ["pf"], ["pf6"])
-    v(1, ts(T.pf[:, 7:8], pl, ph, 16.0, A.add, A.mult), ["pf"], ["pf7"])
-    v(1, ts(T.o3f[:, 0:1], pu, 304.0, T.pf[:, 7:8], A.mult, A.add), ["pf", "pf7"], ["o3a"])
-    v(1, ts(T.o3f[:, 1:2], T.o3f[:, 0:1], 256.0, 639.0, A.add, A.min), ["o3a"], ["o3b"])
-    v(2, cp(T.off3[:], T.o3f[:]), ["o3a", "o3b"], ["off3"])
-    fiota(T.jcol[:, 0:2], [[128, 2]], 0, 1, 2, ["j0"])
-    fiota(T.jcol[:, 2:3], [[0, 1]], CH[2], 1, 1, ["j1"])
-    o1 = []
+    v(64, ts(T.keep[:], T.htab[:], 0.0, LOWEST, A.is_equal, A.mult), ["htab"], ["keep"])
+    lin(64, T.vtab[:, 0:64], T.gtab[:], 8.0, -8.0, ["gtab"], ["vt0"])
+    v(128, tt(T.vtab[:, 192:256], T.vtab[:, 0:64], T.htab[:], A.is_equal), ["vt0", "htab"], ["vt3"])
+    for c in range(3):
+        lin(64, blk(T.vtab, c, 64), T.vtab[:, 192:256], 10240.0, -1280.0, ["vt3"], ["vt%d" % c])
+        lin(8, T.vtab[:, 64 * c + 7:64 * c + 64:8], c8, -1280.0, col(13 + c, pp, 1.0, CH[c] + 8960 - DROP), ["t16", "pf%d" % (13 + c)], ["vt%d" % c])
     for q in range(4):
         q1, q0 = q >> 1, q & 1
-        s1, s0 = 32 - 64 * q1, 64 - 128 * q0
-        for c in range(3):
-            o1.append("o1_%d_%d" % (q, c))
-            if c < 2:
-                fiota(T.o1i[32 * q:32 * q + 32, 8 * c:8 * c + 8], [[s1, 2], [s0, 2], [1, 2]],
-                      32 * q1 + 64 * q0 + 8 * c + 2 * q, 0, 8, o1[-1:])
-            else:
-                fiota(T.o1i[32 * q:32 * q + 32, 16:20], [[s0, 2], [1, 2]], 32 * (1 - q1) + 64 * q0 + 16 + 2 * q, 0, 4, o1[-1:])
+        fiota(T.o1i[32 * q:32 * q + 32, 0:8], [[48 - 96 * q1, 2], [96 - 192 * q0, 2], [1, 2]], 48 * q1 + 96 * q0 + 2 * q, 0, 8, ["o1_%d" % q], q == 1)
+    lin(4, T.o1i[:, 8:12], T.o1i[:, 4:8], 1.0, 8.0, ["o1_%d" % q for q in range(4)], ["o1_4"])
+    lin(8, T.o1i[:, 12:20], T.o1i[:, 0:8], 1.0, 16.0, ["o1_%d" % q for q in range(4)], ["o1_5"])
+    o1 = ["o1_%d" % q for q in range(6)]
     v(20, cp(T.off1[:], T.o1i[:]), o1, ["off1"])
-    fiota(T.utab[:], [[0, 10], [1, 2]], 0, 0, 20, ["utab"])
-    v(20, ts(T.utab[:], T.utab[:], T.pf[:, 4:5], T.pf[:, 5:6], A.mult, A.add), ["utab", "pf4", "pf5"], ["utab"])
-    v(40, tt(T.o2f[:], T.utab[:], T.o1i[:], A.add), o1 + ["utab"], ["o2f"])
-    v(20, cp(T.off2[:], T.o2f[:]), ["o2f"], ["off2"])
-    fiota(T.base[:, 0:NA], [[16, NA]], 15, 0, NA, ["base0"])
-    fiota(T.base[:, NA:20], [[0, NV]], 159, 0, NV, ["base1"])
-    v(20, ts(T.base[:], T.base[:], T.pf[:, 6:7], None, A.add), ["base0", "base1", "pf6"], ["base0", "base1"])
-    fiota(T.tri[:], [[0, 20], [1, 16]], 0, 0, C, ["tri"])
-    v(160, ts(T.tri[:], T.tri[:], pl, None, A.is_gt), ["tri", "pf"], ["tri"])
-    v(64, fill(T.ss[:, 192:256], 0.0), [], ["sspad"])
-    v(32, fill(T.zv[:, 24:32], 0.0), [], ["zvpad"])
-    v(352, fill(T.wo[:], 0.0), [], ["wo"])
+    fiota(T.utab[:], [[0, 10], [1, 2]], 0, 0, 20, ["utab"], True)
+    lin(20, T.utab[:], T.utab[:], col(8, ph, -416.0, 223.0), col(9, ph, 193.0, 0.0), ["pf8", "pf9"], ["utab"])
+    v(32, fill(T.o2f[:], 0.0), [], ["o2f"])
+    v(40, tt(T.o2f[:, 0:20], T.utab[:], T.o1i[:], A.add), o1 + ["utab"], ["o2f"])
+    v(20, cp(T.off2[:], T.o2f[:, 0:20]), ["o2f"], ["off2"])
+    v(168, ts(T.kc[:], T.t16[:], pl, LIFT, A.is_equal, A.mult), ["t16", "pf"], ["kc"])
+    v(64, tt(T.o3f[:], T.o2f[:], T.kc[:, 0:32], A.mult), ["kc", "o2f"], ["o3f"])
+    for k in range(2):
+        a(16, act(blk(T.o3f, k, 16), blk(T.o3f, k, 16), F.Identity, scale=1.0 / LIFT, accum_out=blk(T.o4f, k, 1)), ["o3f"], ["o4f%d" % k])
+    v(2, cp(T.offo[:], T.o4f[:]), ["o4f0", "o4f1"], ["offo"])
+    v(240, fill(T.ta[:], 0.0), [], ["ta"])
+    v(160, ts(T.tri[:], T.t16[:, 0:C], pl, None, A.is_lt), ["t16", "pf"], ["tri"])
+    a(C, act(T.k16[:], T.t16[:, 0:C], F.Sign), ["t16"], ["k16"])
+    early[0] = 90000
+    lin(C, T.kd[:], T.kc[:, 1:C + 1], -2.0, 0.0, ["kc"], ["kd"])
+    v(2 * C, tt(T.kd[:], T.kd[:], T.kc[:, 0:C], A.add), ["kc"], ["kd"])
+    a(C, act(T.kr[:], T.kd[:]), ["kd"], ["kr"])
+    early[0] = 0
+    back, lower = col(11, T.kc[:, 0:1], 2.0, DROP - LIFT, ["kc"]), col(12, T.kc[:, 0:1], 2.0, -LIFT, ["kc"])
+    fiota(T.base[:], [[16, 20]], 0, 0, 20, ["base"])
+    lin(20, T.base[:], T.base[:], 1.0, pl, ["pf"], ["base"])
+    v(40, tt(T.base[:], T.base[:], T.kd[:, 15:C:16], A.add), ["kd"], ["base"])
+    v(1, fill(T.so[:, 158:160], 0.0), [], ["rs0"])
+    for k, n in enumerate(WIDE):
+        mine = [m for m in LANE if LANE[m][0] == k]
+        lo = 16 * min(m for m in mine if m)
+        v(2 * (n - lo), fill(T.ft[:, 4 * (AT[k] + lo):4 * (AT[k] + n)], 0.0), [], ["ft%d" % m for m in mine])
+    v(8, ts(T.of[:], c8, pg, None, A.is_equal), ["t16", "pf"], ["of"])
+    for k in range(8):
+        lin(64, blk(T.og, k, 64), T.ones[:, 0:64], blk(T.of, k, 1), 0.0, ["ones", "of"], ["og%d" % k])
+    quant(T.qo[:], T.so8[:], T.og[:], ["og%d" % k for k in range(8)], ["qo"])
 
-    def spread(eng, buf, c0, name, src, rs):
-        put, mk = (v, cp) if eng == "v" else (a, act)
-        for lo in (0, 64):
-            put(32, mk(buf[64 - lo:128 - lo, c0 + 32:c0 + 64], src(lo, lo + 64)), rs, ["%s_2_%d" % (name, 64 - lo)])
-        for q in range(4):
-            lo, hi = 32 * q, 32 * (q ^ 1)
-            put(64, mk(buf[hi:hi + 32, c0 + 64:c0 + 128], buf[lo:lo + 32, c0:c0 + 64]),
-                [name + "_0", "%s_2_%d" % (name, 64 * (q >> 1))], ["%s_1_%d" % (name, q ^ 1)])
-        return [name + "_0", name + "_2_0", name + "_2_64"] + ["%s_1_%d" % (name, q) for q in range(4)]
+    def lane(m, lo, hi):
+        k, b = LANE[m]
+        return T.ft[:, 4 * (AT[k] + lo) + b:4 * (AT[k] + hi):4]
 
     for t in range(ROUNDS):
-        lik = [mm(128, T.qt[:, lo:lo + 128], T.st[:, lo:lo + 128], T.qu[:], T.su[:], ["t", "u"]) for lo in CH]
+        for c, lo in enumerate(CH):
+            mm(T.qt[:, lo:lo + 128], T.st[:, lo:lo + 128], T.qu[:], T.su[:], ["t%d" % (c // 2), "uq", "us"], c)
         for b in range(4):
-            d, dn, _ = mm(C, blk(T.qe, b, 128), blk(T.se, b, 128), T.qt[:], T.st[:], ["t", "e%d" % b])
-            a(C, act(blk(T.dp, b, C), d), [], [dn, "dp%d" % b])
-        dma("y", "rep%d" % t, [(T.wd[16 * h:16 * h + 16, :], T.dp[:]) for h in range(8)],
-            ["dp%d" % b for b in range(4)], ["wd"], 22000)
-        for k in range(8):
+            d, dn = unpack(b, T.qt[:], T.st[:], ["t0", "t1"])
+            a(C, act(blk(T.wd, b, C), d), [], [dn, "wd%d" % b])
+        line, wd = [], ["wd%d" % b for b in range(4)]
+        dma("y", "rep%d" % t, [(T.wd[lo:hi, 4 * C * r:4 * C * r + 4 * C], T.wd[(lo + 16 * r) % 128:(hi + 16 * r - 1) % 128 + 1, 0:4 * C])
+                               for r in range(1, 8) for lo, hi in ((0, 128 - 16 * r), (128 - 16 * r, 128))], wd, ["wd"], 16000)
+        for k in range(7):
             for c in range(3):
                 z = 2 * c + k % 2
                 pm, m = blk(T.pm, z, 64), T.pm[:, 64 * z + 63:64 * z + 64]
                 sa, sb = blk(T.sa, c, 64), blk(T.sb, c, 64)
-                cur = T.ps[:, lik[c][2]:lik[c][2] + 64] if k == 0 else sa
-                cr, cw = ([], [lik[c][1]]) if k == 0 else (["sa%d" % c], [])
+                cur = T.ps[:, 512 * c:512 * c + 64] if k == 0 else sa
+                cr, cw = ([], ["b%d" % c]) if k == 0 else (["sa%d" % c], [])
                 e, ge, h8 = blk(T.ee, 8 * c + k, 1), blk(T.ng, 8 * c + k, 1), blk(T.hh, 8 * c + k, 1)
-                en, nn, hn, pn, fn = "ee%d_%d" % (c, k), "n%d_%d" % (c, k), "h%d_%d" % (c, k), "pm%d" % z, "fe%d" % z
-                f8, lt8 = blk(T.fe, z, 8), T.lt[:, 64 * c + 7:64 * c + 64:8]
-                v(64, scan(pm, cur, T.neg[:], LOWEST, A.max, A.max), cr + ["neg"], cw + [pn])
-                a(100, act(blk(T.lt, c, 64), pm, F.Sign, bias=m, scale=-1.0, accum_out=e), [pn], ["lt%d" % c, en])
-                a(100, act(lt8, lt8, F.Identity, scale=-64.0, bias=e, accum_out=h8), [en], ["lt%d" % c, hn])
-                a(100, act(blk(T.lg, c, 8), T.pm[:, 64 * z + 7:64 * z + 64:8], F.Sign, bias=m, scale=-1.0, accum_out=ge),
-                  [pn], ["lg%d" % c, nn])
-                if k < 7:
-                    v(64, ts(blk(T.fl, 2 * z, 64), T.gtab[:], ge, -DEAD, A.is_equal, A.mult), ["gtab", nn], ["fg%d" % z])
-                    v(64, ts(blk(T.fl, 2 * z + 1, 64), T.htab[:], h8, -DEAD, A.is_equal, A.mult), ["htab", hn], ["fh%d" % z])
-                    v(128 if k else 64, tt(sb, cur, blk(T.fl, 2 * z, 64), A.add), cr + ["fg%d" % z], cw + ["sb%d" % c])
-                    v(128, tt(sa, sb, blk(T.fl, 2 * z + 1, 64), A.add), ["fh%d" % z, "sb%d" % c], ["sa%d" % c])
-                else:
-                    early[0] = STAGGER * (2 - c)
-                v(8, ts(f8, T.htab[:, 0:8], h8, None, A.not_equal), ["htab", hn], [fn])
-                early[0] = 0
-                a(8, act(T.sk[:, 64 * c + k:64 * c + 64:8], f8, F.Identity, scale=-GONE, bias=m), [fn, pn], ["sk%d_%d" % (c, k)])
-                a(8, act(T.gk[:, 64 * c + k:64 * c + 64:8], f8, F.Identity, scale=-GONE, bias=ge), [fn, nn], ["gk%d_%d" % (c, k)])
-        allk = [(c, k) for c in range(3) for k in range(8)]
-        v(192, scan(T.ss[:, 0:192], T.keep[:], T.sk[:], LOWEST, A.add, A.max), ["keep"] + ["sk%d_%d" % x for x in allk], ["ss"])
-        v(192, scan(T.sg[:], T.keep[:], T.gk[:], LOWEST, A.add, A.max), ["keep"] + ["gk%d_%d" % x for x in allk], ["sg"])
-        ends, ss = (lambda lo, hi: T.ss[lo:hi, 7:256:8]), ["ss", "sspad"]
-        a(32, act(T.zs[:, 0:32], ends(0, 128)), ss, ["zs_0"])
-        zs = spread("a", T.zs, 0, "zs", ends, ss)
-        v(32, tr(T.ta[:, 0:32], ends(0, 128)), ss, ["ta0"])
-        v(32, tr(T.ta[:, 32:64], ends(0, 128)), ss, ["ta1"])
-        v(32, tr(T.zs[:, 128:160], T.ta[:, 16:48]), ["ta0", "ta1"], ["zh_0"])
-        zh = spread("v", T.zs, 128, "zh", (lambda lo, hi: T.zs[lo:hi, 128:160]), ["zh_0"])
-        a(580, act(T.zb[:], T.zs[:, 0:128].indirect(T.off1[:])), zs + ["off1"], ["zb"])
-        v(C, tr(T.row[:], T.zb[:]), ["zb"], ["row"])
-        v(560, cp(T.lb[:], T.zs[:].indirect(T.off2[:])), zs + zh + ["off2"], ["lb"])
+                en, nn, hn, pn = "ee%d_%d" % (c, k), "n%d_%d" % (c, k), "h%d_%d" % (c, k), "pm%d" % z
+                lt8, fg, fh = T.lt[:, 64 * c + 7:64 * c + 64:8], blk(T.fl, 2 * z, 64), blk(T.fl, 2 * z + 1, 64)
+                step = [
+                    v(64, scan(pm, cur, T.neg[:], LOWEST, A.max, A.max), cr + ["neg"], cw + [pn]),
+                    a(90, act(blk(T.lt, c, 64), pm, F.Sign, bias=m, scale=-1.0, accum_out=e), [pn], ["lt%d" % c, en]),
+                    a(90, act(lt8, lt8, F.Identity, scale=-64.0, bias=e, accum_out=h8), [en], ["lt%d" % c, hn]),
+                    a(90, act(blk(T.lg, c, 8), T.pm[:, 64 * z + 7:64 * z + 64:8], F.Sign, bias=m, scale=-1.0, accum_out=ge), [pn], ["lg%d" % c, nn]),
+                    v(64, ts(fg, T.gtab[:], ge, DEAD + k * STEP, A.is_equal, A.mult), ["gtab", nn], ["fg%d" % z]),
+                    v(64, ts(fh, T.htab[:], h8, DEAD - k * STEP, A.is_equal, A.mult), ["htab", hn], ["fh%d" % z]),
+                    v(128 if k else 64, tt(sb, cur, fg, A.subtract), cr + ["fg%d" % z], cw + ["sb%d" % c]),
+                    v(128, tt(sa, sb, fh, A.subtract), ["fh%d" % z, "sb%d" % c], ["sa%d" % c])]
+                line += [(ops[i]["eng"], 3 * k + c + lag, place, i) for i, (lag, place) in zip(step, TURNS)]
+        line.sort()
+        for x, y in zip(line, line[1:]):
+            if x[0] == y[0]:
+                ops[y[3]]["soft"].add(x[3])
         for c in range(3):
-            v(8, ts(blk(T.zv, c, 8), T.sg[:, 64 * c + 7:64 * c + 64:8], 1280.0, blk(T.jcol, c, 1), A.mult, A.add),
-              ["sg", "j0", "j1"], ["zv%d" % c])
-        op(None, 0, None, ["zv0", "zv1", "zv2", "zvpad"], ["zv_0"])
-        zv = spread("a", T.zv, 0, "zv", (lambda lo, hi: T.zv[lo:hi, 0:32]), ["zv_0"])
-        a(580, act(T.zc[:], T.zv[:].indirect(T.off1[:])), zv + ["zv0", "zv1", "zv2", "off1"], ["zc"])
-        v(C, tr(T.val[:], T.zc[:]), ["zc"], ["val"])
-        v(2 * C, tt(T.eq[:], T.row[:], T.lb[:], A.is_equal), ["row", "lb"], ["eq"])
-        v(160, scan(T.cor[:], T.eq[:], T.tri[:], 0.0, A.add, A.mult), ["eq", "tri"], ["cor"])
-        v(40, tt(T.cb[:], T.base[:], T.cor[:, 15:C:16], A.subtract), ["base0", "base1", "cor"], ["cb"])
-        for m in range(20):
-            cut, own = 16 * m + 16, blk(T.lb, 16 * m, 1)
-            if m < NA:
-                o = C * m
-                fore, hind = T.sn[:, o:o + cut], T.sn[:, o + cut:o + C]
-                a(C, act(blk(T.sn, m, C), T.row[:], F.Sign, bias=own, scale=-1.0), ["row", "lb"], ["sna%d" % m, "snb%d" % m])
-                a(cut + 25, act(fore, fore, F.Relu, accum_out=blk(T.a1, m, 1)), [], ["sna%d" % m, "a1_%d" % m])
-                a(C - cut + 25, act(hind, hind, F.Relu, scale=-1.0, accum_out=blk(T.a2, m, 1)), [], ["snb%d" % m, "a2_%d" % m])
+            ab, pen, sk = blk(T.ab, c, 64), blk(T.pen, c, 64), blk(T.sk, c, 64)
+            a(150, act(ab, blk(T.sa, c, 64).indirect(T.offp[:]), F.Abs, bias=DEAD), ["sa%d" % c, "offp"], ["ab%d" % c])
+            v(64, ts(pen, ab, DEAD, -GONE, A.not_equal, A.mult), ["ab%d" % c], ["pen%d" % c])
+            v(64, tt(sk, T.ps[:, 512 * c + 64:512 * c + 128], pen, A.add), ["pen%d" % c], ["b%d" % c, "sk%d" % c])
+            early[0] = STAGGER * (2 - c)
+            v(64, scan(blk(T.sv, c, 64), T.keep[:], sk, LOWEST, A.add, A.max), ["keep", "sk%d" % c], ["ss%d" % c])
+            early[0] = 0
+            v(64, scan(blk(T.sv, 3 + c, 64), pen, blk(T.vtab, c, 64), -DROP, A.max, A.add), ["vt%d" % c, "pen%d" % c], ["sg%d" % c])
+        ss = ["%s%d" % (x, c) for x in ("ss", "sg") for c in range(3)]
+        move("v", 48, T.zs[:, 0:48], T.sv[:, 7:384:8], ss, ["zs0"])
+        for lo, eng in ((0, "a"), (64, "v")):
+            move(eng, 48, T.zs[64 - lo:128 - lo, 48:96], T.sv[lo:lo + 64, 7:384:8], ss, ["zs1_%d" % (64 - lo)])
+        for q in range(4):
+            lo, hi = 32 * q, 32 * (q ^ 1)
+            move("av"[q % 2], 96, T.zs[hi:hi + 32, 96:192], T.zs[lo:lo + 32, 0:96], ["zs0", "zs1_%d" % (64 * (q >> 1))], ["zs2_%d" % q])
+        zs = ["zs0", "zs1_0", "zs1_64"] + ["zs2_%d" % q for q in range(4)]
+        v(192, tr(T.ta[:, 32:224], T.zs[:, 0:192]), zs, ["ta"])
+        v(224, tr(T.zs[:, 192:416], T.ta[:, 16:240]), ["ta"], ["zh"])
+        a(520, act(T.zb[:], T.zs[:, 0:192].indirect(T.off1[:])), zs + ["off1"], ["zb"])
+        v(C, tr(T.row[:], T.zb[:]), ["zb"], ["row"])
+        a(110, act(T.ow[:], T.zs[:].indirect(T.offo[:])), zs + ["zh", "offo"], ["ow"])
+        sums = []
+        v(540, tt(T.eq[:], T.zs[:].indirect(T.off2[:]), T.row[:], A.is_gt), zs + ["zh", "row", "off2"], ["eq"])
+        v(160, scan(lane(0, 0, C), T.tri[:], T.eq[:], 0.0, A.max, A.mult), ["eq", "tri"], ["ft0"])
+        v(160, scan(T.cor[:], T.k16[:], lane(0, 0, C), 0.0, A.mult, A.add), ["k16", "ft0"], ["cor"])
+        v(40, tt(T.cb[:], T.base[:], T.cor[:, 15:C:16], A.subtract), ["base", "cor"], ["cb"])
+        for m in range(19, 0, -1):
+            cut, own, on = 16 * m, blk(T.ow, m, 1), "ft%d" % m
+            if m >= NV:
+                sn = T.sn[:, C * (m - NV):C * (m - NV) + cut]
+                a(cut, act(sn, T.row[:, 0:cut], F.Sign, bias=own, scale=-1.0), ["row", "ow"], ["sn%d" % m])
+                a(cut + 25, act(lane(m, 0, cut), sn, F.Relu, accum_out=blk(T.a1, m, 1)), ["sn%d" % m], [on, "rs%d" % m])
             else:
-                i = m - NA
-                o = C * i
-                v(cut, ts(T.fv[:, o:o + cut], T.row[:, 0:cut], own, 0.5, A.is_ge, A.subtract), ["row", "lb"], ["fva%d" % i])
-                if cut < C:
-                    v(C - cut, ts(T.fv[:, o + cut:o + C], T.row[:, cut:C], own, 0.5, A.is_gt, A.subtract), ["row", "lb"], ["fvb%d" % i])
-                v(80, scan(blk(T.so, i, 160), blk(T.fv, 2 * i, 160), blk(T.fv, 2 * i + 1, 160), 0.0, A.add, A.add),
-                  ["fva%d" % i, "fvb%d" % i], ["so%d" % i])
-        v(16, tt(T.a3[:], T.a2[:], T.a1[:], A.subtract), ["a%d_%d" % (x, m) for x in (1, 2) for m in range(NA)], ["a3"])
-        v(16, tt(T.rk[:, 0:NA], T.a3[:], T.cb[:, 0:NA], A.add), ["a3", "cb"], ["rka"])
-        v(24, tt(T.rk[:, NA:20], T.so[:, 159:160 * NV:160], T.cb[:, NA:20], A.add), ["cb"] + ["so%d" % i for i in range(NV)], ["rkv"])
-        v(20, cp(T.offr[:], T.rk[:]), ["rka", "rkv"], ["offr"])
+                v(cut, ts(lane(m, 0, cut), T.row[:, 0:cut], own, None, A.is_lt), ["row", "ow"], [on])
+                sums.append(v(cut // 4, scan(T.so[:, 160 * m + 160 - cut // 2:160 * m + 160], lane(m, 0, cut // 2), lane(m, cut // 2, cut),
+                                             0.0, A.add, A.add), [on], ["rs%d" % m]))
+        op("a", 560, act(T.zc[:], T.zs[:, 24:192].indirect(T.off1[:])), zs + ["off1"], ["zc"], soft=[writer["rs%d" % m] for m in range(NV, 20)])
+        for k in ORDER:
+            q, sc = T.qf[:, AT[k]:AT[k] + WIDE[k]], T.sf[:, AT[k]:AT[k] + WIDE[k]]
+            done = quant(q, sc, T.ft[:, 4 * AT[k]:4 * (AT[k] + WIDE[k])], ["ft%d" % m for m in LANE if LANE[m][0] == k], ["qf%d" % k])
+            mm(T.qo[:], T.so8[:], q, sc, ["qo", "qf%d" % k], 0, k == ORDER[0], k == ORDER[-1])
+        for i in (v(40, tt(T.kr[:, 15:16 * NV:16], T.cb[:, 0:NV], T.so[:, 159:160 * NV:160], A.subtract),
+                    ["cb"] + ["rs%d" % m for m in range(NV)], ["krv"]),
+                  v(40, tt(T.kr[:, 16 * NV + 15:C:16], T.cb[:, NV:20], T.a1[:, NV:20], A.subtract),
+                    ["cb"] + ["rs%d" % m for m in range(NV, 20)], ["kra"]),
+                  v(C, tr(T.val[:], T.zc[:]), ["zc"], ["val"])):
+            ops[i]["soft"].add(done)
+        v(C, scan(T.dr[:], T.ps[:, 0:C], T.kr[:], -2 * LIFT, A.max, A.add), ["krv", "kra", "kr"], ["b0", "dr"])
+        v(20, ts(T.offr[:], T.dr[:, 15:C:16], lower, None, A.add), ["dr", "pf12"], ["offr"])
         v(1250, cp(T.wo[:].indirect(T.offr[:]), T.val[:]), ["offr", "val"], ["wo"])
-        v(C, tr(T.tt[:, 0:C], T.wo[:, 0:C]), ["wo"], ["tt0"])
-        v(C, tr(T.tt[:, C:2 * C], T.wo[:, 16:16 + C]), ["wo"], ["tt1"])
-        v(110, cp(T.offb[:], T.tt[:].indirect(T.off3[:])), ["tt0", "tt1", "off3"], ["offb"])
+        v(C, scan(T.dg[:], T.wo[:], T.kd[:], -2 * LIFT, A.max, A.add), ["wo", "kd"], ["dg"])
+        v(20, ts(T.offb[:], T.dg[:, 15:C:16], back, None, A.add), ["dg", "pf11"], ["offb"])
         for b in range(4):
-            put, mk = (v, cp) if b < 2 else (a, act)
-            put(570, mk(T.bt[:, b:4 * C:4], T.wd[:, C * b:32 * C].indirect(T.offb[:, 0:20])), ["wd", "offb"], ["bt%d" % b])
+            move("vvaa"[b], 540, T.bt[:, b:4 * C:4], T.wd[:, C * b:32 * C].indirect(T.offb[:]), wd + ["wd", "offb"], ["bt%d" % b])
         qb, sq, qm, sm = T["qb%d" % t], T["sq%d" % t], T["qm%d" % t], T["sm%d" % t]
-        quant(qb[:], sq[:], T.bt[:], C, ["bt%d" % b for b in range(4)], ["qb%d" % t])
+        quant(qb[:], sq[:], T.bt[:], ["bt%d" % b for b in range(4)], ["qb%d" % t])
 
         def deal(t=t, qb=qb, sq=sq, qm=qm, sm=sm):
-            for kind in (0, 1):
-                tf = []
-                for d in range(1, N):
-                    j = (rank + d) % N
-                    rid, pid = topo.addr(T.cores[j], core)
-                    eng = topo.engines(core, T.cores[j])
-                    src, dst = (u8(blk(qb, j, L)), u8(blk(qm, rank, L))) if kind == 0 else (blk(sq, j, L), blk(sm, rank, L))
-                    tf.append(RemoteDMATransfer(dst_ids=[DstId(rid=rid, pnc=pid)], dma_engine_mask=1 << eng[d - 1 + kind],
-                                                remote_sem=T.sem["arr%d" % t], src=src, dst=dst))
+            to = [(rank + d) % N for d in range(1, N)]
+            far = topo.engines(core, T.cores[to[0]])
+            tf = [transfer(topo, core, T.cores[j], far[d:d + 1], T.sem["arr%d" % t], u8(blk(qb, j, L)), u8(blk(qm, rank, L)))
+                  for d, j in enumerate(to)]
+            if HELP:
+                for k, c in enumerate(helpers(core, T, topo)):
+                    rest = [e for e in topo.engines(core, c) if e not in far]
+                    tf.append(transfer(topo, core, c, rest[4 * k:4 * k + 4], T.sem["hin%d" % t], blk(sq, k, 4 * L), T["hl%d" % t][:]))
                 g.remote_dma_fused(tf, local_sem=T.sem["snd%d" % t])
-        sent = op("g", 1500, deal, ["qb%d" % t], [], sem="snd%d" % t, inc=2 * (N - 1), lat=6000)
-        op(None, 0, None, [], ["marr%d" % t], sem="arr%d" % t, inc=2 * (N - 1), after=[sent])
+            else:
+                g.remote_dma_fused(tf, local_sem=T.sem["snd%d" % t])
+                g.remote_dma_fused([transfer(topo, core, T.cores[j], far[d + 1:d + 2], T.sem["arr%d" % t], blk(sq, j, L), blk(sm, rank, L))
+                                    for d, j in enumerate(to)], local_sem=T.sem["snd%d" % t])
+        sent = op("g", 1500, deal, ["qb%d" % t], [], sem="snd%d" % t, inc=N - 1 + 8 if HELP else 2 * (N - 1), lat=6000)
+        op(None, 0, None, [], ["marr%d" % t], sem="arr%d" % t, inc=(3 if HELP else 2) * (N - 1), after=[sent])
         dma("y", "own%d" % t, [(u8(blk(qm, rank, L)), u8(blk(qb, rank, L))), (blk(sm, rank, L), blk(sq, rank, L))],
             ["qb%d" % t], ["mown%d" % t], 2400)
         if t == ROUNDS - 1:
-            v(336, ts(T.t1[:], T.wo[:, 0:336], 1.0 / 1280, None, A.mult), ["wo", "qb%d" % t], ["t1"])
-            v(336, cp(T.t2[:], T.t1[:]), ["t1"], ["t2"])
-            v(336, ts(T.t3[:], T.t2[:], -1280.0, None, A.mult), ["t2"], ["t3"])
-            v(672, tt(T.oo[:], T.t3[:], T.wo[:, 0:336], A.add), ["t3", "wo"], ["oo"])
-            v(C, ts(T.g1[:], T.val[:], 1.0 / 1280, None, A.mult), ["val", "qb%d" % t], ["g1"])
-            v(C, cp(T.g2[:], T.g1[:]), ["g1"], ["g2"])
-            v(C, cp(T.g3[:], T.g2[:]), ["g2"], ["g3"])
-            dma("y", "ol1", [(T.ol[0:8:2, 0:C], T.oo[0:128:32, 0:C]), (T.ol[1:8:2, 0:C], T.oo[16:128:32, 16:16 + C])], ["oo"], [], 2400)
+            v(C, ts(T.t1[:], T.wo[:], DROP, 1.0 / 1280, A.add, A.mult), ["wo", "qb%d" % t], ["t1"])
+            v(C, ts(T.t1[:], T.t1[:], WHOLE, WHOLE, A.add, A.subtract), [], ["t1"])
+            v(C, ts(T.t3[:], T.t1[:], -1280.0, DROP, A.mult, A.add), ["t1"], ["t3"])
+            v(2 * C, tt(T.oo[:], T.t3[:], T.wo[:], A.add), ["t3", "wo"], ["oo"])
+            v(C, ts(T.g1[:], T.val[:], DROP, 1.0 / 1280, A.add, A.mult), ["val", "qb%d" % t], ["g1"])
+            v(C, ts(T.g1[:], T.g1[:], WHOLE, WHOLE, A.add, A.subtract), [], ["g1"])
+            v(C, ts(T.g1[:], T.g1[:], pg, None, A.add), ["pf"], ["g1"])
+            v(C, ts(T.g2[:], T.g1[:], 8.0, -8.0, A.is_ge, A.mult), ["g1"], ["g2"])
+            v(2 * C, tt(T.g3[:], T.g1[:], T.g2[:], A.add), ["g1", "g2"], ["g3"])
+            dma("y", "ol1", [(T.ol[:, 0:C], T.oo[0:128:16, :])], ["oo"], [], 2400)
             dma("y", "ol2", [(T.ol[:, C:2 * C], T.g3[0:128:16, :])], ["g3"], [], 2400)
         got = ["marr%d" % t, "mown%d" % t]
-        for b in range(4):
-            w, wn, _ = mm(C, blk(T.qw, b, 128), blk(T.sw, b, 128), qm[:], sm[:], got + ["w"])
-            d, dn, _ = mm(C, blk(T.qe, 4 + b, 128), blk(T.se, 4 + b, 128), qm[:], sm[:], got + ["e%d" % (4 + b)])
-            a(C, act(blk(T.rr, b, C), w, F.Relu, scale=0.03125), [], [wn, "rr%d" % b])
-            v(C, tt(T.xs[:, b:4 * C:4], d, blk(T.rr, b, C), A.add), ["rr%d" % b], [dn, "xs%d" % b])
-        quant(T.qt[:], T.st[:], T.xs[:], C, ["xs%d" % b for b in range(4)], ["t"])
+        for k, (lo, hi) in enumerate(PIECES):
+            n, q, sc = hi - lo, qm[:, lo:hi], sm[:, lo:hi]
+            for b in range(4):
+                rr, x = T.rr[:, C * b + lo:C * b + hi], "%d_%d" % (k, b)
+                w, wn = mm(blk(T.qw, b, 128), blk(T.sw, b, 128), q, sc, got + ["w"], BANKS[k][2 * b])
+                d, dn = unpack(b, q, sc, got, BANKS[k][2 * b + 1])
+                a(n, act(rr, w, F.Relu, scale=0.03125), [], [wn, "rr" + x])
+                v(n, tt(T.xs[:, 4 * lo + b:4 * hi:4], d, rr, A.add), ["rr" + x], [dn, "xs" + x])
+            quant(T.qt[:, lo:hi], T.st[:, lo:hi], T.xs[:, 4 * lo:4 * hi], ["xs%d_%d" % (k, b) for b in range(4)], ["t%d" % k])
 
-    d, dn, _ = mm(C, T.qv[:], T.sv[:], T.qt[:], T.st[:], ["t", "v"])
-    v(C, cp(T.yo[:], d), [], [dn, "yo"])
-    dma("y", "oy", [(T.y[:], T.yo[:])], ["yo"], [], 2400)
+    for k, (lo, hi) in enumerate(PIECES):
+        d, dn = mm(T.qv[:], T.sv8[:], T.qt[:, lo:hi], T.st[:, lo:hi], ["t%d" % k, "v"], k)
+        v(hi - lo, cp(T.yo[:, lo:hi], d), [], [dn, "yo%d" % k])
+    dma("y", "oy", [(T.y[:], T.yo[:])], ["yo0", "yo1"], [], 2400)
     dma("a", "oq", [(T.oc[:], u8(T.qt[:]))] + [(T.osc[4 * k:4 * k + 4, :], T.st[32 * k:32 * k + 4, :]) for k in range(4)],
-        ["t"], [], 2400)
+        ["t0", "t1"], [], 2400)
 
     n = len(ops)
     succ = [[] for _ in range(n)]
@@ -309,14 +374,14 @@ def rank_program(g, core, T, topo):
             succ[d].append(i)
     ahead = [0.0] * n
     for i in range(n - 1, -1, -1):
-        ahead[i] = ops[i]["cost"] + ops[i]["lat"] + ops[i]["early"] + max([ahead[j] + HOP_CROSS for j in succ[i]], default=0)
+        ahead[i] = ops[i]["cost"] + ops[i]["lat"] + ops[i]["early"] + max([ahead[j] + HOP for j in succ[i]], default=0)
     left = [len(o["deps"] | o["soft"]) for o in ops]
     ready_at, free, order = [0.0] * n, {k: 0.0 for k in queue}, []
     ready = [i for i in range(n) if left[i] == 0]
     while ready:
         start = {i: max(ready_at[i], free.get(ops[i]["eng"], 0.0)) for i in ready}
         first = min(ready, key=lambda i: start[i])
-        near = [i for i in ready if ops[i]["eng"] == ops[first]["eng"] and start[i] <= start[first] + 40]
+        near = [i for i in ready if ops[i]["eng"] == ops[first]["eng"] and start[i] <= start[first] + NEAR]
         i = max(near, key=lambda i: ahead[i])
         ready.remove(i)
         order.append(i)
@@ -325,7 +390,7 @@ def rank_program(g, core, T, topo):
         if o["eng"] is not None:
             free[o["eng"]] = end
         for j in succ[i]:
-            hop = 0 if o["eng"] is None or i not in ops[j]["deps"] else (HOP_SAME if ops[j]["eng"] == o["eng"] else HOP_CROSS)
+            hop = 0 if o["eng"] is None or i not in ops[j]["deps"] else HOP
             ready_at[j] = max(ready_at[j], end + o["lat"] + hop)
             left[j] -= 1
             if left[j] == 0:
@@ -337,16 +402,11 @@ def rank_program(g, core, T, topo):
     for i in order:
         o = ops[i]
         if o["eng"] is None:
-            if o["sem"] is not None:
-                count[o["sem"]] += o["inc"]
-                need[i] = [(o["sem"], count[o["sem"]], {})]
-            else:
-                need[i] = [x for d in o["deps"] for x in need[d]]
+            count[o["sem"]] += o["inc"]
+            need[i] = [(o["sem"], count[o["sem"]], {})]
             continue
         kn = known[o["eng"]]
         wants = sorted([x for d in o["deps"] for x in need[d]], key=lambda x: -len(x[2]) * 100000 - x[1])
-        if o["eng"] == "g" and o["sem"] is None:
-            wants.append(("cg", count["cg"], {}))
         for s, c, snap in wants:
             if kn.get(s, 0) < c:
                 kn[s] = max(c2 for s2, c2, _ in wants if s2 == s)

from concourse.bass import DstId, RemoteDMATransfer
from concourse.mybir import dt, AluOpType, ActivationFunctionType

C, L, ROUNDS, N = 320, 40, 3, 8
CH = (0, 64, 192)
PIECES = ((0, 192), (192, C))
BANKS = ((3, 4, 5, 6, 7, 0, 1, 2), (3, 4, 5, 6, 7, 2, 3, 4))
NV = 13
WIDE = (320, 256, 192, 128, 128)
AT = [sum(WIDE[:k]) for k in range(5)]
LANE = {m: ((20 - m) // 4, m % 4) for m in range(1, 20)}
LANE[0] = (0, 0)
ORDER = (0, 4, 3, 2, 1)
HELP = True
DEAD, STEP, GONE, LOWEST = 2.0 ** 98, 2.0 ** 94, 2.0 ** 90, -(2.0 ** 95)
LIFT, DROP, WHOLE = 32768.0, 20480.0, 1.5 * 2 ** 23
_B = {
    "bfloat16": dict(x0=4 * C, ut=512, vt=512, xs=4 * C, ones=516, et=516, wd=32 * C, bt=4 * C, htab=64, gtab=64, t16=C + 16, kc=C + 16, kd=C,
                     tri=C, lt=192, lg=24, fl=768, pen=192, eq=C, cor=C, k16=C, og=512, ft=4096, so=16 * 160, sn=12 * C),
    "float32": dict(rr=4 * C, neg=64, keep=64, vtab=256, pf=24, o1i=20, utab=20, o2f=32, o3f=32, o4f=2, of=8, base=20,
                    pm=384, ee=24, ng=24, hh=24, sa=192, sb=192, ab=192, sk=192, sv=384, ta=240, zs=416, zb=C, row=C, ow=32,
                    zc=C, val=C, kr=C, dr=C, cb=20, a1=20, wo=C, dg=C, t1=C, t3=C, oo=C, g1=C, g2=C, g3=C, yo=C),
    "int32": dict(pi=8),
    "uint16": dict(off1=20, off2=20, offo=2, offu=8, offp=4, offr=20, offb=20),
    "float8_e4m3fn_x4": dict(qu0=128, qu=128, qv=128, qw=512, qt=C, qe=512, qf=1024, qo=128, qb0=C, qb1=C, qb2=C, qm0=C, qm1=C, qm2=C),
    "uint8": dict(su0=128, su=128, sv8=128, sw=512, st=C, se=512, sf=1024, so8=128, sq0=C, sq1=C, sq2=C, sm0=C, sm1=C, sm2=C,
                  hl0=4 * L, hl1=4 * L, hl2=4 * L),
}
SCRATCH = {k: ("sbuf", [128, n], d) for d, bufs in _B.items() for k, n in bufs.items()}
SCRATCH["ps"] = ("psum", [128, 4096], "float32")
SEMAPHORES = (["cv", "ca", "cp", "cg", "lx", "lu", "lw", "lv", "ol1", "ol2", "oy", "oq", "hout"]
              + ["%s%d" % (a, t) for a in ("rep", "own", "snd", "arr", "hin") for t in range(ROUNDS)])

A = AluOpType
F = ActivationFunctionType
HOP, NEAR, STAGGER = 180, 100, 400
TURNS = [(0, 0), (0, 0), (0, 2), (0, 1), (1, 1), (1, 3), (1, 4), (2, 2)]


def u8(view):
    return view.bitcast(dt.uint8)


def blk(buf, k, n):
    return buf[:, n * k:n * k + n]


def transfer(topo, core, to, engines, sem, src, dst):
    rid, pid = topo.addr(to, core)
    return RemoteDMATransfer(dst_ids=[DstId(rid=rid, pnc=pid)], dma_engine_mask=sum(1 << e for e in engines), remote_sem=sem, src=src, dst=dst)


def helpers(core, T, topo):
    free = [c for c in topo.cores_of(core) if T.rank_of(c) is None]
    return sorted(free, key=lambda c: topo.die(c) != topo.die(core))[:2]


def helper_program(g, core, T, topo, rank, half):
    to = [j for j in range(4 * half, 4 * half + 4) if j != rank]
    for t in range(ROUNDS):
        g.wait_ge(T.sem["hin%d" % t], 4)
        g.remote_dma_fused([transfer(topo, core, T.cores[j], topo.engines(core, T.cores[j])[2 * (j % 4):2 * (j % 4) + 2], T.sem["arr%d" % t],
                                     blk(T["hl%d" % t], j % 4, L), blk(T["sm%d" % t], rank, L)) for j in to], local_sem=T.sem.hout)
    g.wait_ge(T.sem.hout, 2 * len(to) * ROUNDS)


def rank_program(g, core, T, topo):
    rank = T.rank_of(core)
    if rank is None:
        for r, c in enumerate(T.cores):
            if HELP and core in helpers(c, T, topo):
                helper_program(g, core, T, topo, r, helpers(c, T, topo).index(core))
        return
    V, S, P, Y = g.vector, g.scalar, g.tensor, g.sync
    queue = {"v": V, "a": S, "p": P, "g": g, "y": Y}
    ops, writer, readers, early, mms, gs = [], {}, {}, [0], [], []

    def op(eng, cost, fn, r=(), w=(), sem=None, inc=0, lat=0, after=(), soft=()):
        deps = set(after) | {writer[k] for k in list(r) + list(w) if k in writer}
        for k in w:
            deps.update(readers.get(k, ()))
        i = len(ops)
        for k in r:
            readers.setdefault(k, []).append(i)
        for k in w:
            writer[k] = i
            readers[k] = []
        ops.append({"eng": eng, "cost": cost, "fn": fn, "deps": deps, "sem": sem, "inc": inc,
                    "early": early[0], "soft": set(soft), "lat": lat})
        return i

    def v(n, fn, r, w):
        return op("v", max(64, n) + 10, fn, r, w)

    def a(n, fn, r, w):
        return op("a", max(64, n) + 40, fn, r, w)

    def dma(eng, sem, pairs, r, w, lat):
        def fn():
            for o, i in pairs:
                queue[eng].dma_start(o, i).then_inc(T.sem[sem], 16)
        return op(eng, 100 * len(pairs), fn, r, w, sem=sem, inc=16 * len(pairs), lat=lat)

    def mm(lq, ls, rq, rs, r, bank=None, start=True, stop=True):
        n = rq.shape[1]
        bank = 3 + len(mms) % 5 if bank is None else bank
        out, name = T.ps[:, 512 * bank:512 * bank + n], "b%d" % bank
        mms.append(op("p", 1.3 * n + 60, lambda: P.matmul_mx(out, lq, ls, rq, rs, start, stop), r, [name] if start else [], soft=mms[-1:]))
        writer[name] = mms[-1]
        return out, name

    def quant(q, s, src, r, w):
        return op("v", 20 + 1.1 * q.shape[1], lambda: V.quantize_mx(q, s, src), r, w)

    def ts(out, in0, s1, s2, *o):
        return lambda: V.tensor_scalar(out, in0, s1, s2, *o)

    def tt(out, i0, i1, o):
        return lambda: V.tensor_tensor(out, i0, i1, o)

    def cp(out, in_):
        return lambda: V.tensor_copy(out, in_)

    def act(out, in_, func=F.Copy, **kw):
        return lambda: S.activation(out, in_, func, **kw)

    def scan(out, d0, d1, init, o0, o1):
        return lambda: V.tensor_tensor_scan(out, d0, d1, init, o0, o1)

    def tr(out, in_):
        return lambda: V.transpose(out, in_)

    def fill(out, x):
        return lambda: V.memset(out, x)

    def move(eng, n, out, in_, r, w):
        return v(n, cp(out, in_), r, w) if eng == "v" else a(n, act(out, in_), r, w)

    def lin(n, out, in_, scale, bias, r, w):
        a(n, act(out, in_, F.Identity, scale=scale, bias=bias), r, w)

    def iota(out, pat, base, cm, n, w, wait=False, **kw):
        gs.append(op("g", 160 + 2 * n, lambda: g.iota(out, pat, base, cm, **kw), [], w, soft=gs[-1:], after=gs[-1:] if wait else []))

    def fiota(out, pat, base, cm, n, w, wait=False):
        iota(out, pat, base, cm, n, w, wait, allow_small_or_imprecise_dtypes=True)

    dma("y", "lx", [(T.x0[:], T.x[:])], [], ["x0"], 3200)
    dma("a", "lu", [(T.ut[:], T.u[:])], [], ["ut"], 2600)
    dma("y", "lw", [(u8(T.qw[:]), T.wc[:]), (T.sw[:], T.ws[:])], [], ["w"], 9000)
    dma("y", "lv", [(T.vt[:], T.v[:])], [], ["vt"], 30000)
    quant(T.qt[:], T.st[:], T.x0[:], ["x0"], ["t0", "t1"])
    quant(T.qu0[:], T.su0[:], T.ut[:], ["ut"], ["u0"])
    quant(T.qv[:], T.sv8[:], T.vt[:], ["vt"], ["v"])

    iota(T.pi[:, 0:1], [[0, 1]], 0, 1, 1, ["pi0"])
    fiota(T.t16[:], [[0, 21], [1, 16]], 0, 0, C + 16, ["t16"])
    v(258, fill(T.ones[:], 1.0), [], ["ones"])
    gs.append(op("g", 1240, lambda: g.affine_select(T.et[:], T.ones[:], [[1, 516]], A.is_equal, 0.0, -3, -4), ["ones"], ["et"], soft=gs[-1:]))
    for b in range(4):
        quant(blk(T.qe, b, 128), blk(T.se, b, 128), T.et[:, 3 - b:515 - b], ["et"], ["e%d" % b])

    def unpack(b, q, s, rs, bank=None):
        return mm(blk(T.qe, b, 128), blk(T.se, b, 128), q, s, rs + ["e%d" % b], bank)
    fiota(T.htab[:], [[0, 8], [8, 8]], 0, 0, 64, ["htab"])
    fiota(T.gtab[:], [[1, 8], [0, 8]], 0, 0, 64, ["gtab"])
    for k, (sh, mask) in enumerate([(0, 15), (4, 1), (3, 1), (0, 7), (4, 7)]):
        v(1, ts(blk(T.pi, k + 1, 1), T.pi[:, 0:1], sh, mask, A.logical_shift_right, A.bitwise_and), ["pi0"], ["pi%d" % (k + 1)])
    v(6, cp(T.pf[:, 16:22], T.pi[:, 0:6]), ["pi%d" % k for k in range(6)], ["pf"])
    pp, pl, ph, p8, p7, pg = [blk(T.pf, k, 1) for k in range(16, 22)]
    c4, c8 = T.t16[:, 0:4], T.t16[:, 0:8]

    def col(k, in_, scale, bias, r=()):
        lin(1, blk(T.pf, k, 1), in_, scale, bias, ["pf"] + list(r), ["pf%d" % k])
        return blk(T.pf, k, 1)
    v(4, ts(T.offu[:, 0:4], c4, 32.0, col(5, p8, 16.0, p7), A.mult, A.add), ["t16", "pf5"], ["offu0"])
    v(4, ts(T.offu[:, 4:8], c4, 2.0, col(6, p7, 16.0, p8), A.mult, A.add), ["t16", "pf6"], ["offu1"])
    v(4, ts(T.offp[:], c4, 2.0, col(7, p7, 8.0, p8), A.mult, A.add), ["t16", "pf7"], ["offp"])
    v(250, cp(T.qu[:].bitcast(dt.uint32), T.qu0[:].bitcast(dt.uint32).indirect(T.offu[:])), ["u0", "offu0", "offu1"], ["uq"])
    a(250, act(T.su[:], T.su0[:].indirect(T.offu[:])), ["u0", "offu0", "offu1"], ["us"])
    v(64, fill(T.neg[:], LOWEST), [], ["neg"])
    v(64, ts(T.keep[:], T.htab[:], 0.0, LOWEST, A.is_equal, A.mult), ["htab"], ["keep"])
    lin(64, T.vtab[:, 0:64], T.gtab[:], 8.0, -8.0, ["gtab"], ["vt0"])
    v(128, tt(T.vtab[:, 192:256], T.vtab[:, 0:64], T.htab[:], A.is_equal), ["vt0", "htab"], ["vt3"])
    for c in range(3):
        lin(64, blk(T.vtab, c, 64), T.vtab[:, 192:256], 10240.0, -1280.0, ["vt3"], ["vt%d" % c])
        lin(8, T.vtab[:, 64 * c + 7:64 * c + 64:8], c8, -1280.0, col(13 + c, pp, 1.0, CH[c] + 8960 - DROP), ["t16", "pf%d" % (13 + c)], ["vt%d" % c])
    for q in range(4):
        q1, q0 = q >> 1, q & 1
        fiota(T.o1i[32 * q:32 * q + 32, 0:8], [[48 - 96 * q1, 2], [96 - 192 * q0, 2], [1, 2]], 48 * q1 + 96 * q0 + 2 * q, 0, 8, ["o1_%d" % q], q == 1)
    lin(4, T.o1i[:, 8:12], T.o1i[:, 4:8], 1.0, 8.0, ["o1_%d" % q for q in range(4)], ["o1_4"])
    lin(8, T.o1i[:, 12:20], T.o1i[:, 0:8], 1.0, 16.0, ["o1_%d" % q for q in range(4)], ["o1_5"])
    o1 = ["o1_%d" % q for q in range(6)]
    v(20, cp(T.off1[:], T.o1i[:]), o1, ["off1"])
    fiota(T.utab[:], [[0, 10], [1, 2]], 0, 0, 20, ["utab"], True)
    lin(20, T.utab[:], T.utab[:], col(8, ph, -416.0, 223.0), col(9, ph, 193.0, 0.0), ["pf8", "pf9"], ["utab"])
    v(32, fill(T.o2f[:], 0.0), [], ["o2f"])
    v(40, tt(T.o2f[:, 0:20], T.utab[:], T.o1i[:], A.add), o1 + ["utab"], ["o2f"])
    v(20, cp(T.off2[:], T.o2f[:, 0:20]), ["o2f"], ["off2"])
    v(168, ts(T.kc[:], T.t16[:], pl, LIFT, A.is_equal, A.mult), ["t16", "pf"], ["kc"])
    v(64, tt(T.o3f[:], T.o2f[:], T.kc[:, 0:32], A.mult), ["kc", "o2f"], ["o3f"])
    for k in range(2):
        a(16, act(blk(T.o3f, k, 16), blk(T.o3f, k, 16), F.Identity, scale=1.0 / LIFT, accum_out=blk(T.o4f, k, 1)), ["o3f"], ["o4f%d" % k])
    v(2, cp(T.offo[:], T.o4f[:]), ["o4f0", "o4f1"], ["offo"])
    v(240, fill(T.ta[:], 0.0), [], ["ta"])
    v(160, ts(T.tri[:], T.t16[:, 0:C], pl, None, A.is_lt), ["t16", "pf"], ["tri"])
    a(C, act(T.k16[:], T.t16[:, 0:C], F.Sign), ["t16"], ["k16"])
    early[0] = 90000
    lin(C, T.kd[:], T.kc[:, 1:C + 1], -2.0, 0.0, ["kc"], ["kd"])
    v(2 * C, tt(T.kd[:], T.kd[:], T.kc[:, 0:C], A.add), ["kc"], ["kd"])
    a(C, act(T.kr[:], T.kd[:]), ["kd"], ["kr"])
    early[0] = 0
    back, lower = col(11, T.kc[:, 0:1], 2.0, DROP - LIFT, ["kc"]), col(12, T.kc[:, 0:1], 2.0, -LIFT, ["kc"])
    fiota(T.base[:], [[16, 20]], 0, 0, 20, ["base"])
    lin(20, T.base[:], T.base[:], 1.0, pl, ["pf"], ["base"])
    v(40, tt(T.base[:], T.base[:], T.kd[:, 15:C:16], A.add), ["kd"], ["base"])
    v(1, fill(T.so[:, 158:160], 0.0), [], ["rs0"])
    for k, n in enumerate(WIDE):
        mine = [m for m in LANE if LANE[m][0] == k]
        lo = 16 * min(m for m in mine if m)
        v(2 * (n - lo), fill(T.ft[:, 4 * (AT[k] + lo):4 * (AT[k] + n)], 0.0), [], ["ft%d" % m for m in mine])
    v(8, ts(T.of[:], c8, pg, None, A.is_equal), ["t16", "pf"], ["of"])
    for k in range(8):
        lin(64, blk(T.og, k, 64), T.ones[:, 0:64], blk(T.of, k, 1), 0.0, ["ones", "of"], ["og%d" % k])
    quant(T.qo[:], T.so8[:], T.og[:], ["og%d" % k for k in range(8)], ["qo"])

    def lane(m, lo, hi):
        k, b = LANE[m]
        return T.ft[:, 4 * (AT[k] + lo) + b:4 * (AT[k] + hi):4]

    for t in range(ROUNDS):
        for c, lo in enumerate(CH):
            mm(T.qt[:, lo:lo + 128], T.st[:, lo:lo + 128], T.qu[:], T.su[:], ["t%d" % (c // 2), "uq", "us"], c)
        for b in range(4):
            d, dn = unpack(b, T.qt[:], T.st[:], ["t0", "t1"])
            a(C, act(blk(T.wd, b, C), d), [], [dn, "wd%d" % b])
        line, wd = [], ["wd%d" % b for b in range(4)]
        dma("y", "rep%d" % t, [(T.wd[lo:hi, 4 * C * r:4 * C * r + 4 * C], T.wd[(lo + 16 * r) % 128:(hi + 16 * r - 1) % 128 + 1, 0:4 * C])
                               for r in range(1, 8) for lo, hi in ((0, 128 - 16 * r), (128 - 16 * r, 128))], wd, ["wd"], 16000)
        for k in range(7):
            for c in range(3):
                z = 2 * c + k % 2
                pm, m = blk(T.pm, z, 64), T.pm[:, 64 * z + 63:64 * z + 64]
                sa, sb = blk(T.sa, c, 64), blk(T.sb, c, 64)
                cur = T.ps[:, 512 * c:512 * c + 64] if k == 0 else sa
                cr, cw = ([], ["b%d" % c]) if k == 0 else (["sa%d" % c], [])
                e, ge, h8 = blk(T.ee, 8 * c + k, 1), blk(T.ng, 8 * c + k, 1), blk(T.hh, 8 * c + k, 1)
                en, nn, hn, pn = "ee%d_%d" % (c, k), "n%d_%d" % (c, k), "h%d_%d" % (c, k), "pm%d" % z
                lt8, fg, fh = T.lt[:, 64 * c + 7:64 * c + 64:8], blk(T.fl, 2 * z, 64), blk(T.fl, 2 * z + 1, 64)
                step = [
                    v(64, scan(pm, cur, T.neg[:], LOWEST, A.max, A.max), cr + ["neg"], cw + [pn]),
                    a(90, act(blk(T.lt, c, 64), pm, F.Sign, bias=m, scale=-1.0, accum_out=e), [pn], ["lt%d" % c, en]),
                    a(90, act(lt8, lt8, F.Identity, scale=-64.0, bias=e, accum_out=h8), [en], ["lt%d" % c, hn]),
                    a(90, act(blk(T.lg, c, 8), T.pm[:, 64 * z + 7:64 * z + 64:8], F.Sign, bias=m, scale=-1.0, accum_out=ge), [pn], ["lg%d" % c, nn]),
                    v(64, ts(fg, T.gtab[:], ge, DEAD + k * STEP, A.is_equal, A.mult), ["gtab", nn], ["fg%d" % z]),
                    v(64, ts(fh, T.htab[:], h8, DEAD - k * STEP, A.is_equal, A.mult), ["htab", hn], ["fh%d" % z]),
                    v(128 if k else 64, tt(sb, cur, fg, A.subtract), cr + ["fg%d" % z], cw + ["sb%d" % c]),
                    v(128, tt(sa, sb, fh, A.subtract), ["fh%d" % z, "sb%d" % c], ["sa%d" % c])]
                line += [(ops[i]["eng"], 3 * k + c + lag, place, i) for i, (lag, place) in zip(step, TURNS)]
        line.sort()
        for x, y in zip(line, line[1:]):
            if x[0] == y[0]:
                ops[y[3]]["soft"].add(x[3])
        for c in range(3):
            ab, pen, sk = blk(T.ab, c, 64), blk(T.pen, c, 64), blk(T.sk, c, 64)
            a(150, act(ab, blk(T.sa, c, 64).indirect(T.offp[:]), F.Abs, bias=DEAD), ["sa%d" % c, "offp"], ["ab%d" % c])
            v(64, ts(pen, ab, DEAD, -GONE, A.not_equal, A.mult), ["ab%d" % c], ["pen%d" % c])
            v(64, tt(sk, T.ps[:, 512 * c + 64:512 * c + 128], pen, A.add), ["pen%d" % c], ["b%d" % c, "sk%d" % c])
            early[0] = STAGGER * (2 - c)
            v(64, scan(blk(T.sv, c, 64), T.keep[:], sk, LOWEST, A.add, A.max), ["keep", "sk%d" % c], ["ss%d" % c])
            early[0] = 0
            v(64, scan(blk(T.sv, 3 + c, 64), pen, blk(T.vtab, c, 64), -DROP, A.max, A.add), ["vt%d" % c, "pen%d" % c], ["sg%d" % c])
        ss = ["%s%d" % (x, c) for x in ("ss", "sg") for c in range(3)]
        move("v", 48, T.zs[:, 0:48], T.sv[:, 7:384:8], ss, ["zs0"])
        for lo, eng in ((0, "a"), (64, "v")):
            move(eng, 48, T.zs[64 - lo:128 - lo, 48:96], T.sv[lo:lo + 64, 7:384:8], ss, ["zs1_%d" % (64 - lo)])
        for q in range(4):
            lo, hi = 32 * q, 32 * (q ^ 1)
            move("av"[q % 2], 96, T.zs[hi:hi + 32, 96:192], T.zs[lo:lo + 32, 0:96], ["zs0", "zs1_%d" % (64 * (q >> 1))], ["zs2_%d" % q])
        zs = ["zs0", "zs1_0", "zs1_64"] + ["zs2_%d" % q for q in range(4)]
        v(192, tr(T.ta[:, 32:224], T.zs[:, 0:192]), zs, ["ta"])
        v(224, tr(T.zs[:, 192:416], T.ta[:, 16:240]), ["ta"], ["zh"])
        a(520, act(T.zb[:], T.zs[:, 0:192].indirect(T.off1[:])), zs + ["off1"], ["zb"])
        v(C, tr(T.row[:], T.zb[:]), ["zb"], ["row"])
        a(110, act(T.ow[:], T.zs[:].indirect(T.offo[:])), zs + ["zh", "offo"], ["ow"])
        sums = []
        v(540, tt(T.eq[:], T.zs[:].indirect(T.off2[:]), T.row[:], A.is_gt), zs + ["zh", "row", "off2"], ["eq"])
        v(160, scan(lane(0, 0, C), T.tri[:], T.eq[:], 0.0, A.max, A.mult), ["eq", "tri"], ["ft0"])
        v(160, scan(T.cor[:], T.k16[:], lane(0, 0, C), 0.0, A.mult, A.add), ["k16", "ft0"], ["cor"])
        v(40, tt(T.cb[:], T.base[:], T.cor[:, 15:C:16], A.subtract), ["base", "cor"], ["cb"])
        for m in range(19, 0, -1):
            cut, own, on = 16 * m, blk(T.ow, m, 1), "ft%d" % m
            if m >= NV:
                sn = T.sn[:, C * (m - NV):C * (m - NV) + cut]
                a(cut, act(sn, T.row[:, 0:cut], F.Sign, bias=own, scale=-1.0), ["row", "ow"], ["sn%d" % m])
                a(cut + 25, act(lane(m, 0, cut), sn, F.Relu, accum_out=blk(T.a1, m, 1)), ["sn%d" % m], [on, "rs%d" % m])
            else:
                v(cut, ts(lane(m, 0, cut), T.row[:, 0:cut], own, None, A.is_lt), ["row", "ow"], [on])
                sums.append(v(cut // 4, scan(T.so[:, 160 * m + 160 - cut // 2:160 * m + 160], lane(m, 0, cut // 2), lane(m, cut // 2, cut),
                                             0.0, A.add, A.add), [on], ["rs%d" % m]))
        op("a", 560, act(T.zc[:], T.zs[:, 24:192].indirect(T.off1[:])), zs + ["off1"], ["zc"], soft=[writer["rs%d" % m] for m in range(NV, 20)])
        for k in ORDER:
            q, sc = T.qf[:, AT[k]:AT[k] + WIDE[k]], T.sf[:, AT[k]:AT[k] + WIDE[k]]
            done = quant(q, sc, T.ft[:, 4 * AT[k]:4 * (AT[k] + WIDE[k])], ["ft%d" % m for m in LANE if LANE[m][0] == k], ["qf%d" % k])
            mm(T.qo[:], T.so8[:], q, sc, ["qo", "qf%d" % k], 0, k == ORDER[0], k == ORDER[-1])
        for i in (v(40, tt(T.kr[:, 15:16 * NV:16], T.cb[:, 0:NV], T.so[:, 159:160 * NV:160], A.subtract),
                    ["cb"] + ["rs%d" % m for m in range(NV)], ["krv"]),
                  v(40, tt(T.kr[:, 16 * NV + 15:C:16], T.cb[:, NV:20], T.a1[:, NV:20], A.subtract),
                    ["cb"] + ["rs%d" % m for m in range(NV, 20)], ["kra"]),
                  v(C, tr(T.val[:], T.zc[:]), ["zc"], ["val"])):
            ops[i]["soft"].add(done)
        v(C, scan(T.dr[:], T.ps[:, 0:C], T.kr[:], -2 * LIFT, A.max, A.add), ["krv", "kra", "kr"], ["b0", "dr"])
        v(20, ts(T.offr[:], T.dr[:, 15:C:16], lower, None, A.add), ["dr", "pf12"], ["offr"])
        v(1250, cp(T.wo[:].indirect(T.offr[:]), T.val[:]), ["offr", "val"], ["wo"])
        v(C, scan(T.dg[:], T.wo[:], T.kd[:], -2 * LIFT, A.max, A.add), ["wo", "kd"], ["dg"])
        v(20, ts(T.offb[:], T.dg[:, 15:C:16], back, None, A.add), ["dg", "pf11"], ["offb"])
        for b in range(4):
            move("vvaa"[b], 540, T.bt[:, b:4 * C:4], T.wd[:, C * b:32 * C].indirect(T.offb[:]), wd + ["wd", "offb"], ["bt%d" % b])
        qb, sq, qm, sm = T["qb%d" % t], T["sq%d" % t], T["qm%d" % t], T["sm%d" % t]
        quant(qb[:], sq[:], T.bt[:], ["bt%d" % b for b in range(4)], ["qb%d" % t])

        def deal(t=t, qb=qb, sq=sq, qm=qm, sm=sm):
            to = [(rank + d) % N for d in range(1, N)]
            far = topo.engines(core, T.cores[to[0]])
            tf = [transfer(topo, core, T.cores[j], far[d:d + 1], T.sem["arr%d" % t], u8(blk(qb, j, L)), u8(blk(qm, rank, L)))
                  for d, j in enumerate(to)]
            if HELP:
                for k, c in enumerate(helpers(core, T, topo)):
                    rest = [e for e in topo.engines(core, c) if e not in far]
                    tf.append(transfer(topo, core, c, rest[4 * k:4 * k + 4], T.sem["hin%d" % t], blk(sq, k, 4 * L), T["hl%d" % t][:]))
                g.remote_dma_fused(tf, local_sem=T.sem["snd%d" % t])
            else:
                g.remote_dma_fused(tf, local_sem=T.sem["snd%d" % t])
                g.remote_dma_fused([transfer(topo, core, T.cores[j], far[d + 1:d + 2], T.sem["arr%d" % t], blk(sq, j, L), blk(sm, rank, L))
                                    for d, j in enumerate(to)], local_sem=T.sem["snd%d" % t])
        sent = op("g", 1500, deal, ["qb%d" % t], [], sem="snd%d" % t, inc=N - 1 + 8 if HELP else 2 * (N - 1), lat=6000)
        op(None, 0, None, [], ["marr%d" % t], sem="arr%d" % t, inc=(3 if HELP else 2) * (N - 1), after=[sent])
        dma("y", "own%d" % t, [(u8(blk(qm, rank, L)), u8(blk(qb, rank, L))), (blk(sm, rank, L), blk(sq, rank, L))],
            ["qb%d" % t], ["mown%d" % t], 2400)
        if t == ROUNDS - 1:
            v(C, ts(T.t1[:], T.wo[:], DROP, 1.0 / 1280, A.add, A.mult), ["wo", "qb%d" % t], ["t1"])
            v(C, ts(T.t1[:], T.t1[:], WHOLE, WHOLE, A.add, A.subtract), [], ["t1"])
            v(C, ts(T.t3[:], T.t1[:], -1280.0, DROP, A.mult, A.add), ["t1"], ["t3"])
            v(2 * C, tt(T.oo[:], T.t3[:], T.wo[:], A.add), ["t3", "wo"], ["oo"])
            v(C, ts(T.g1[:], T.val[:], DROP, 1.0 / 1280, A.add, A.mult), ["val", "qb%d" % t], ["g1"])
            v(C, ts(T.g1[:], T.g1[:], WHOLE, WHOLE, A.add, A.subtract), [], ["g1"])
            v(C, ts(T.g1[:], T.g1[:], pg, None, A.add), ["pf"], ["g1"])
            v(C, ts(T.g2[:], T.g1[:], 8.0, -8.0, A.is_ge, A.mult), ["g1"], ["g2"])
            v(2 * C, tt(T.g3[:], T.g1[:], T.g2[:], A.add), ["g1", "g2"], ["g3"])
            dma("y", "ol1", [(T.ol[:, 0:C], T.oo[0:128:16, :])], ["oo"], [], 2400)
            dma("y", "ol2", [(T.ol[:, C:2 * C], T.g3[0:128:16, :])], ["g3"], [], 2400)
        got = ["marr%d" % t, "mown%d" % t]
        for k, (lo, hi) in enumerate(PIECES):
            n, q, sc = hi - lo, qm[:, lo:hi], sm[:, lo:hi]
            for b in range(4):
                rr, x = T.rr[:, C * b + lo:C * b + hi], "%d_%d" % (k, b)
                w, wn = mm(blk(T.qw, b, 128), blk(T.sw, b, 128), q, sc, got + ["w"], BANKS[k][2 * b])
                d, dn = unpack(b, q, sc, got, BANKS[k][2 * b + 1])
                a(n, act(rr, w, F.Relu, scale=0.03125), [], [wn, "rr" + x])
                v(n, tt(T.xs[:, 4 * lo + b:4 * hi:4], d, rr, A.add), ["rr" + x], [dn, "xs" + x])
            quant(T.qt[:, lo:hi], T.st[:, lo:hi], T.xs[:, 4 * lo:4 * hi], ["xs%d_%d" % (k, b) for b in range(4)], ["t%d" % k])

    for k, (lo, hi) in enumerate(PIECES):
        d, dn = mm(T.qv[:], T.sv8[:], T.qt[:, lo:hi], T.st[:, lo:hi], ["t%d" % k, "v"], k)
        v(hi - lo, cp(T.yo[:, lo:hi], d), [], [dn, "yo%d" % k])
    dma("y", "oy", [(T.y[:], T.yo[:])], ["yo0", "yo1"], [], 2400)
    dma("a", "oq", [(T.oc[:], u8(T.qt[:]))] + [(T.osc[4 * k:4 * k + 4, :], T.st[32 * k:32 * k + 4, :]) for k in range(4)],
        ["t0", "t1"], [], 2400)

    n = len(ops)
    succ = [[] for _ in range(n)]
    for i, o in enumerate(ops):
        for d in o["deps"] | o["soft"]:
            succ[d].append(i)
    ahead = [0.0] * n
    for i in range(n - 1, -1, -1):
        ahead[i] = ops[i]["cost"] + ops[i]["lat"] + ops[i]["early"] + max([ahead[j] + HOP for j in succ[i]], default=0)
    left = [len(o["deps"] | o["soft"]) for o in ops]
    ready_at, free, order = [0.0] * n, {k: 0.0 for k in queue}, []
    ready = [i for i in range(n) if left[i] == 0]
    while ready:
        start = {i: max(ready_at[i], free.get(ops[i]["eng"], 0.0)) for i in ready}
        first = min(ready, key=lambda i: start[i])
        near = [i for i in ready if ops[i]["eng"] == ops[first]["eng"] and start[i] <= start[first] + NEAR]
        i = max(near, key=lambda i: ahead[i])
        ready.remove(i)
        order.append(i)
        o = ops[i]
        end = start[i] + o["cost"]
        if o["eng"] is not None:
            free[o["eng"]] = end
        for j in succ[i]:
            hop = 0 if o["eng"] is None or i not in ops[j]["deps"] else HOP
            ready_at[j] = max(ready_at[j], end + o["lat"] + hop)
            left[j] -= 1
            if left[j] == 0:
                ready.append(j)

    count = {k: 0 for k in SEMAPHORES}
    known = {k: {} for k in queue}
    need = [None] * n
    for i in order:
        o = ops[i]
        if o["eng"] is None:
            count[o["sem"]] += o["inc"]
            need[i] = [(o["sem"], count[o["sem"]], {})]
            continue
        kn = known[o["eng"]]
        wants = sorted([x for d in o["deps"] for x in need[d]], key=lambda x: -len(x[2]) * 100000 - x[1])
        for s, c, snap in wants:
            if kn.get(s, 0) < c:
                kn[s] = max(c2 for s2, c2, _ in wants if s2 == s)
                queue[o["eng"]].wait_ge(T.sem[s], kn[s])
            for s2, c2 in snap.items():
                kn[s2] = max(kn.get(s2, 0), c2)
        if o["sem"] is None:
            s = "c" + o["eng"]
            o["fn"]().then_inc(T.sem[s], 1)
            count[s] += 1
        else:
            s = o["sem"]
            o["fn"]()
            count[s] += o["inc"]
        need[i] = [(s, count[s], dict(kn))]
    for s in SEMAPHORES:
        if count[s]:
            g.wait_ge(T.sem[s], count[s])
